import numpy as np
import ml_dtypes


def mxq(x, axis, fmt="e4m3"):
    dtype, down = {"e4m3": (ml_dtypes.float8_e4m3fn, 7), "e5m2": (ml_dtypes.float8_e5m2, 14)}[fmt]
    v = np.moveaxis(np.asarray(x, np.float32).astype(ml_dtypes.bfloat16).astype(np.float64), axis, -1)
    blocks = v.reshape(v.shape[:-1] + (-1, 32))
    amax = np.abs(blocks).max(-1, keepdims=True)
    byte = np.maximum(np.where(amax > 0, np.frexp(amax)[1] - 1 + 127, 0) - down, 1)
    scale = np.exp2(byte - 127.0)
    codes = (blocks / scale).astype(np.float32).astype(dtype).astype(np.float64)
    return np.moveaxis((codes * scale).reshape(v.shape), -1, axis)


WIDE = False


def mx_kscale(k):
    if not WIDE:
        return np.ones(k)
    levels = np.array([10, -10, 5, -5, 0])
    if k % 512:
        return np.exp2(np.random.permutation(np.resize(levels, k // 32))).repeat(32)
    a = np.empty((k // 512, 16))
    for p in range(k // 512):
        a[p, :8] = np.random.permutation(np.resize(levels, 8))
        for g in range(8):
            far = levels[np.abs(levels - a[p, g]) >= 10]
            a[p, g + 8] = far[np.random.randint(len(far))]
    return np.exp2(a.ravel()).repeat(32)


def f64(x):
    return np.asarray(x).astype(np.float64)


def striped(idx):
    return np.tile(np.asarray(idx).reshape(-1, 16).T, (8, 1)).astype(np.uint16)


def unstriped(offs):
    return offs[:16].T.reshape(-1).astype(np.int64)


B, N, C, D, NQ = 1, 256, 512, 512, 512


def eight(codes):
    return np.concatenate([codes[h].reshape(-1, 16).T for h in range(8)]).astype(np.uint16)


def uneight(offs):
    return np.stack([offs[16 * h:16 * h + 16].T.reshape(-1) for h in range(8)]).astype(np.int64)


def setup_inputs():
    n = np.random.standard_normal
    s = mx_kscale(D)[:, None]
    grid = lambda x: np.round(x * 32) / 32
    return {
        "qT": (n((B, D, NQ)) * s / np.sqrt(D)).astype(np.float32),
        "cb": (grid(n((D, C))) / s).astype(np.float32),
        "norm": np.tile(np.random.randint(32, 129, N) / 64.0, (128, 1)).astype(np.float32),
        "offs": eight(np.random.randint(0, C, (8, N))),
    }


def reference(qT, cb, norm, offs):
    k = []
    for part, offs_ in enumerate((offs,)):
        codes = uneight(offs_)
        k += [f64(cb)[512 * part + 64 * h:512 * part + 64 * h + 64][:, codes[h]] for h in range(8)]
    k = np.concatenate(k) * f64(norm)[:1]
    a = mxq(f64(qT), 1, "e4m3").transpose(0, 2, 1) @ mxq(k, 0, "e4m3")
    return a

@@ -1,0 +1,154 @@
+from contextlib import ExitStack
+
+import concourse.mybir as mybir
+
+D, C, N, Q = 512, 512, 256, 512
+
+F32 = mybir.dt.float32
+BF16 = mybir.dt.bfloat16
+U16 = mybir.dt.uint16
+U32 = mybir.dt.uint32
+U8 = mybir.dt.uint8
+FP8X4 = mybir.dt.float8_e4m3fn_x4
+MULT = mybir.AluOpType.mult
+P = 128
+T = 4
+FLOPS = 2 * D * Q * N
+
+
+def tile_attend_pq_lin_kernel(tc, qT, cb, norm, offs, out):
+    nc = tc.nc
+    with ExitStack() as ctx:
+        keep = ctx.enter_context(tc.tile_pool(name="keep", bufs=1))
+        psum = ctx.enter_context(tc.psum_pool(name="psum", bufs=1))
+        offsets = keep.tile([P, N // 16], U16, name="offsets")
+        norm_h = [keep.tile([P, 128], F32, name=f"norm{h}") for h in range(2)]
+        cb_rows = cb.rearrange("(p t) c -> p t c", t=T)
+        books = [keep.tile([P, C], F32, name=f"book{t}") for t in range(T)]
+        q_rows = qT[0].rearrange("(p t) q -> p t q", t=T)
+        q_cuts = [[0,256],[256,512]]
+        raws = [keep.tile([P, T, b - a], F32, name=f"raw{a}") for a, b in q_cuts]
+
+        def ld_offs():
+            nc.sync.dma_start(offsets[:], offs)
+
+        def ld_norm(h):
+            nc.sync.dma_start(norm_h[h][:], norm[:, 128 * h : 128 * h + 128])
+
+        def ld_cb(t):
+            nc.sync.dma_start(books[t][:], cb_rows[:, t, :])
+
+        def ld_q(i):
+            a, b = q_cuts[i]
+            nc.sync.dma_start(raws[i][:], q_rows[:, :, a:b])
+
+        dummy = keep.tile([P, 1], F32, name="dummy")
+        dummy2 = keep.tile([P, 1], F32, name="dummy2")
+        nc.gpsimd.memset(dummy[:], 0.0)
+        nc.scalar.copy(out=dummy2[:], in_=dummy[:])
+
+        ks = keep.tile([P, T, N], F32, name="ks")
+        kb = keep.tile([P, N, T], BF16, name="kb", align_bytes=64)
+        k_codes = keep.tile([P, N], U32, name="k_codes", align_bytes=64)
+        k_scales = keep.tile([P, N], U8, name="k_scales", align_bytes=64)
+        qb = [keep.tile([P, P, T], BF16, name=f"qb{m}", align_bytes=64) for m in range(4)]
+        q_codes = [keep.tile([P, P], U32, name=f"q_codes{m}", align_bytes=64) for m in range(4)]
+        q_scales = [keep.tile([P, P], U8, name=f"q_scales{m}", align_bytes=64) for m in range(4)]
+
+        def weave(copy, dst, src):
+            copy(
+                out=dst.rearrange("p (c i) t -> p c t i", i=4),
+                in_=src.rearrange("p t (c i) -> p c t i", i=4),
+            )
+
+        engines = {"v": nc.vector.tensor_copy, "s": nc.scalar.copy, "g": nc.gpsimd.tensor_copy}
+
+        def gather_half(t, h):
+            cols = slice(128 * h, 128 * h + 128)
+            nc.vector.tensor_tensor(
+                ks[:, t, cols], books[t][:].indirect(offsets[:, 8 * h : 8 * h + 8]), norm_h[h][:], MULT)
+
+        def ki(e, a, b):
+            weave(engines[e], kb[:, a:b, :], ks[:, :, a:b])
+
+        def kq(a, b):
+            nc.vector.quantize_mx(
+                out=k_codes[:, a:b].bitcast(FP8X4), scales=k_scales[:, a:b],
+                in_=kb[:, a:b, :].rearrange("p c t -> p (c t)"))
+
+        def qi(e, m, a, b):
+            lo = 128 * m + a
+            for i, (x, y) in enumerate(q_cuts):
+                if x <= lo < y:
+                    weave(engines[e], qb[m][:, a:b, :], raws[i][:, :, lo - x : lo - x + b - a])
+
+        def qq(m):
+            nc.vector.quantize_mx(
+                out=q_codes[m][:].bitcast(FP8X4), scales=q_scales[m][:],
+                in_=qb[m][:].rearrange("p c t -> p (c t)"))
+
+        out_rows = out[0].rearrange("(m p) n -> m p n", p=P)
+        accs = {}
+        ress = {}
+
+        def mm(m, a=0, b=N):
+            acc = psum.tile([P, b - a], F32, name=f"acc{m}_{a}")
+            accs[(m, a)] = acc
+            nc.tensor.matmul_mx(
+                out=acc[:],
+                lhsT=q_codes[m][:].bitcast(FP8X4), lhsT_scale=q_scales[m][:],
+                rhs=k_codes[:, a:b].bitcast(FP8X4), rhs_scale=k_scales[:, a:b],
+                start=True, stop=True)
+
+        def ev(e, m, a=0, b=N):
+            if m not in ress:
+                ress[m] = keep.tile([P, N], F32, name=f"res{m}")
+            engines[e](out=ress[m][:, a:b], in_=accs[(m, a)][:])
+
+        def st(m, q="sync"):
+            (nc.sync if q == "sync" else nc.scalar).dma_start(out_rows[m], ress[m][:])
+
+        ld_offs()
+        ld_norm(0)
+        ld_cb(0)
+        ld_norm(1)
+        ld_cb(1)
+        ld_cb(2)
+        ld_cb(3)
+        ld_q(0)
+        ld_q(1)
+        qi("s", 0, 0, 128)
+        qi("s", 1, 0, 128)
+        qi("s", 2, 0, 96)
+        gather_half(0, 0)
+        gather_half(0, 1)
+        gather_half(1, 0)
+        gather_half(1, 1)
+        gather_half(2, 0)
+        gather_half(2, 1)
+        gather_half(3, 0)
+        gather_half(3, 1)
+        ki("v", 0, 128)
+        ki("v", 128, 256)
+        kq(0, 128)
+        kq(128, 256)
+        qq(0)
+        mm(0)
+        qi("v", 3, 0, 128)
+        qq(1)
+        mm(1)
+        qi("v", 2, 96, 128)
+        qq(3)
+        mm(3)
+        qq(2)
+        mm(2, 0, 128)
+        mm(2, 128, 256)
+        ev("s", 0)
+        st(0)
+        ev("v", 1)
+        st(1)
+        ev("s", 3)
+        st(3)
+        ev("v", 2, 0, 128)
+        ev("v", 2, 128, 256)
+        st(2)

@@ -108,9 +108,9 @@ def tile_attend_pq_lin_kernel(tc, qT, cb, norm, offs, out):
         def st(m, q="sync"):
             (nc.sync if q == "sync" else nc.scalar).dma_start(out_rows[m], ress[m][:])
 
-        ld_offs()
-        ld_norm(0)
         ld_cb(0)
+        ld_norm(0)
+        ld_offs()
         ld_norm(1)
         ld_cb(1)
         ld_cb(2)

@@ -22,7 +22,10 @@ def tile_attend_pq_lin_kernel(tc, qT, cb, norm, offs, out):
         keep = ctx.enter_context(tc.tile_pool(name="keep", bufs=1))
         psum = ctx.enter_context(tc.psum_pool(name="psum", bufs=1))
         offsets = keep.tile([P, N // 16], U16, name="offsets")
-        norm_h = [keep.tile([P, 128], F32, name=f"norm{h}") for h in range(2)]
+        norm_t = keep.tile([P, N], F32, name="norm_t", align_bytes=64)
+        norm_rows = keep.tile([P, 32], F32, name="norm_rows", align_bytes=64)
+        norm_cols = keep.tile([P, 32], F32, name="norm_cols", align_bytes=64)
+        norm_wide = keep.tile([P, N], F32, name="norm_wide", align_bytes=64)
         cb_rows = cb.rearrange("(p t) c -> p t c", t=T)
         books = [keep.tile([P, C], F32, name=f"book{t}") for t in range(T)]
         q_rows = qT[0].rearrange("(p t) q -> p t q", t=T)
@@ -32,8 +35,17 @@ def tile_attend_pq_lin_kernel(tc, qT, cb, norm, offs, out):
         def ld_offs():
             nc.sync.dma_start(offsets[:], offs)
 
-        def ld_norm(h):
-            nc.sync.dma_start(norm_h[h][:], norm[:, 128 * h : 128 * h + 128])
+        def ld_norm(queue):
+            queue.dma_start(norm_rows[:], norm[0:16, :].rearrange("r (b y) -> (r b) y", y=32))
+
+        def spread_norm():
+            nc.vector.transpose(norm_cols[:], norm_rows[:])
+            for h in range(2):
+                nc.vector.tensor_copy(
+                    out=norm_wide[:, 128 * h : 128 * h + 128].rearrange("p (b x) -> p b x", x=32),
+                    in_=norm_cols[:, 4 * h : 4 * h + 4].unsqueeze(2).to_broadcast([P, 4, 32]))
+            for h in range(2):
+                nc.vector.transpose(norm_t[:, 128 * h : 128 * h + 128], norm_wide[:, 128 * h : 128 * h + 128])
 
         def ld_cb(t):
             nc.sync.dma_start(books[t][:], cb_rows[:, t, :])
@@ -66,7 +78,7 @@ def tile_attend_pq_lin_kernel(tc, qT, cb, norm, offs, out):
         def gather_half(t, h):
             cols = slice(128 * h, 128 * h + 128)
             nc.vector.tensor_tensor(
-                ks[:, t, cols], books[t][:].indirect(offsets[:, 8 * h : 8 * h + 8]), norm_h[h][:], MULT)
+                ks[:, t, cols], books[t][:].indirect(offsets[:, 8 * h : 8 * h + 8]), norm_t[:, cols], MULT)
 
         def ki(e, a, b):
             weave(engines[e], kb[:, a:b, :], ks[:, :, a:b])
@@ -108,15 +120,15 @@ def tile_attend_pq_lin_kernel(tc, qT, cb, norm, offs, out):
         def st(m, q="sync"):
             (nc.sync if q == "sync" else nc.scalar).dma_start(out_rows[m], ress[m][:])
 
+        ld_norm(nc.sync)
         ld_cb(0)
-        ld_norm(0)
         ld_offs()
-        ld_norm(1)
         ld_cb(1)
         ld_cb(2)
         ld_cb(3)
         ld_q(0)
         ld_q(1)
+        spread_norm()
         qi("s", 0, 0, 128)
         qi("s", 1, 0, 128)
         qi("s", 2, 0, 96)

@@ -80,6 +80,9 @@ def tile_attend_pq_lin_kernel(tc, qT, cb, norm, offs, out):
             nc.vector.tensor_tensor(
                 ks[:, t, cols], books[t][:].indirect(offsets[:, 8 * h : 8 * h + 8]), norm_t[:, cols], MULT)
 
+        def gather(t):
+            nc.vector.tensor_tensor(ks[:, t, :], books[t][:].indirect(offsets[:]), norm_t[:], MULT)
+
         def ki(e, a, b):
             weave(engines[e], kb[:, a:b, :], ks[:, :, a:b])
 
@@ -117,8 +120,8 @@ def tile_attend_pq_lin_kernel(tc, qT, cb, norm, offs, out):
                 ress[m] = keep.tile([P, N], F32, name=f"res{m}")
             engines[e](out=ress[m][:, a:b], in_=accs[(m, a)][:])
 
-        def st(m, q="sync"):
-            (nc.sync if q == "sync" else nc.scalar).dma_start(out_rows[m], ress[m][:])
+        def st(m, a=0, b=N):
+            nc.sync.dma_start(out_rows[m][:, a:b], ress[m][:, a:b])
 
         ld_norm(nc.sync)
         ld_cb(0)
@@ -131,13 +134,11 @@ def tile_attend_pq_lin_kernel(tc, qT, cb, norm, offs, out):
         spread_norm()
         qi("s", 0, 0, 128)
         qi("s", 1, 0, 128)
-        qi("s", 2, 0, 96)
+        qi("s", 3, 0, 96)
         gather_half(0, 0)
         gather_half(0, 1)
-        gather_half(1, 0)
-        gather_half(1, 1)
-        gather_half(2, 0)
-        gather_half(2, 1)
+        gather(1)
+        gather(2)
         gather_half(3, 0)
         gather_half(3, 1)
         ki("v", 0, 128)
@@ -146,21 +147,23 @@ def tile_attend_pq_lin_kernel(tc, qT, cb, norm, offs, out):
         kq(128, 256)
         qq(0)
         mm(0)
-        qi("v", 3, 0, 128)
         qq(1)
         mm(1)
-        qi("v", 2, 96, 128)
+        qi("v", 3, 96, 128)
+        qi("v", 2, 0, 128)
         qq(3)
-        mm(3)
+        mm(3, 0, 128)
+        mm(3, 128, 256)
         qq(2)
         mm(2, 0, 128)
         mm(2, 128, 256)
         ev("s", 0)
         st(0)
-        ev("v", 1)
+        ev("s", 1)
         st(1)
-        ev("s", 3)
+        ev("v", 3, 0, 128)
+        ev("s", 3, 128, 256)
         st(3)
         ev("v", 2, 0, 128)
-        ev("v", 2, 128, 256)
+        ev("s", 2, 128, 256)
         st(2)

@@ -11,6 +11,7 @@ U32 = mybir.dt.uint32
 U8 = mybir.dt.uint8
 FP8X4 = mybir.dt.float8_e4m3fn_x4
 MULT = mybir.AluOpType.mult
+COPY = mybir.ActivationFunctionType.Copy
 P = 128
 T = 4
 FLOPS = 2 * D * Q * N
@@ -59,6 +60,7 @@ def tile_attend_pq_lin_kernel(tc, qT, cb, norm, offs, out):
         nc.gpsimd.memset(dummy[:], 0.0)
         nc.scalar.copy(out=dummy2[:], in_=dummy[:])
 
+        picked = {}
         ks = keep.tile([P, T, N], F32, name="ks")
         kb = keep.tile([P, N, T], BF16, name="kb", align_bytes=64)
         k_codes = keep.tile([P, N], U32, name="k_codes", align_bytes=64)
@@ -82,6 +84,15 @@ def tile_attend_pq_lin_kernel(tc, qT, cb, norm, offs, out):
 
         def gather(t):
             nc.vector.tensor_tensor(ks[:, t, :], books[t][:].indirect(offsets[:]), norm_t[:], MULT)
+
+        def scalar_gather(t):
+            book16 = keep.tile([P, C], BF16, name=f"book16_{t}")
+            picked[t] = keep.tile([P, N], BF16, name=f"picked{t}")
+            nc.scalar.activation(book16[:], books[t][:], COPY)
+            nc.scalar.activation(picked[t][:], book16[:].indirect(offsets[:]), COPY)
+
+        def scale(t):
+            nc.vector.tensor_tensor(ks[:, t, :], picked[t][:], norm_t[:], MULT)
 
         def ki(e, a, b):
             weave(engines[e], kb[:, a:b, :], ks[:, :, a:b])
@@ -123,8 +134,8 @@ def tile_attend_pq_lin_kernel(tc, qT, cb, norm, offs, out):
         def st(m, a=0, b=N):
             nc.sync.dma_start(out_rows[m][:, a:b], ress[m][:, a:b])
 
-        ld_norm(nc.sync)
         ld_cb(0)
+        ld_norm(nc.sync)
         ld_offs()
         ld_cb(1)
         ld_cb(2)
@@ -132,13 +143,14 @@ def tile_attend_pq_lin_kernel(tc, qT, cb, norm, offs, out):
         ld_q(0)
         ld_q(1)
         spread_norm()
+        scalar_gather(1)
         qi("s", 0, 0, 128)
         qi("s", 1, 0, 128)
         qi("s", 3, 0, 96)
         gather_half(0, 0)
         gather_half(0, 1)
-        gather(1)
         gather(2)
+        scale(1)
         gather_half(3, 0)
         gather_half(3, 1)
         ki("v", 0, 128)

@@ -12,8 +12,16 @@ U8 = mybir.dt.uint8
 FP8X4 = mybir.dt.float8_e4m3fn_x4
 MULT = mybir.AluOpType.mult
 COPY = mybir.ActivationFunctionType.Copy
+
 P = 128
-T = 4
+PLANES = 4
+BLOCK = 32
+LIST_ROWS = 16
+RUN = 4
+HALVES = (slice(0, N // 2), slice(N // 2, N))
+Q_LOAD = Q // 2
+SCALAR_PLANE = 1
+SCALAR_SHARE = 96
 FLOPS = 2 * D * Q * N
 
 
@@ -22,160 +30,110 @@ def tile_attend_pq_lin_kernel(tc, qT, cb, norm, offs, out):
     with ExitStack() as ctx:
         keep = ctx.enter_context(tc.tile_pool(name="keep", bufs=1))
         psum = ctx.enter_context(tc.psum_pool(name="psum", bufs=1))
-        offsets = keep.tile([P, N // 16], U16, name="offsets")
+        offsets = keep.tile([P, N // LIST_ROWS], U16, name="offsets")
         norm_t = keep.tile([P, N], F32, name="norm_t", align_bytes=64)
-        norm_rows = keep.tile([P, 32], F32, name="norm_rows", align_bytes=64)
-        norm_cols = keep.tile([P, 32], F32, name="norm_cols", align_bytes=64)
+        norm_rows = keep.tile([P, BLOCK], F32, name="norm_rows", align_bytes=64)
+        norm_cols = keep.tile([P, BLOCK], F32, name="norm_cols", align_bytes=64)
         norm_wide = keep.tile([P, N], F32, name="norm_wide", align_bytes=64)
-        cb_rows = cb.rearrange("(p t) c -> p t c", t=T)
-        books = [keep.tile([P, C], F32, name=f"book{t}") for t in range(T)]
-        q_rows = qT[0].rearrange("(p t) q -> p t q", t=T)
-        q_cuts = [[0,256],[256,512]]
-        raws = [keep.tile([P, T, b - a], F32, name=f"raw{a}") for a, b in q_cuts]
+        books = [keep.tile([P, C], F32, name=f"book{t}") for t in range(PLANES)]
+        raws = [keep.tile([P, PLANES, Q_LOAD], F32, name=f"raw{a}") for a in range(0, Q, Q_LOAD)]
 
-        def ld_offs():
-            nc.sync.dma_start(offsets[:], offs)
-
-        def ld_norm(queue):
-            queue.dma_start(norm_rows[:], norm[0:16, :].rearrange("r (b y) -> (r b) y", y=32))
-
-        def spread_norm():
-            nc.vector.transpose(norm_cols[:], norm_rows[:])
-            for h in range(2):
-                nc.vector.tensor_copy(
-                    out=norm_wide[:, 128 * h : 128 * h + 128].rearrange("p (b x) -> p b x", x=32),
-                    in_=norm_cols[:, 4 * h : 4 * h + 4].unsqueeze(2).to_broadcast([P, 4, 32]))
-            for h in range(2):
-                nc.vector.transpose(norm_t[:, 128 * h : 128 * h + 128], norm_wide[:, 128 * h : 128 * h + 128])
-
-        def ld_cb(t):
-            nc.sync.dma_start(books[t][:], cb_rows[:, t, :])
-
-        def ld_q(i):
-            a, b = q_cuts[i]
-            nc.sync.dma_start(raws[i][:], q_rows[:, :, a:b])
-
-        dummy = keep.tile([P, 1], F32, name="dummy")
-        dummy2 = keep.tile([P, 1], F32, name="dummy2")
-        nc.gpsimd.memset(dummy[:], 0.0)
-        nc.scalar.copy(out=dummy2[:], in_=dummy[:])
-
-        picked = {}
-        ks = keep.tile([P, T, N], F32, name="ks")
-        kb = keep.tile([P, N, T], BF16, name="kb", align_bytes=64)
+        ks = keep.tile([P, PLANES, N], F32, name="ks")
+        kb = keep.tile([P, N, PLANES], BF16, name="kb", align_bytes=64)
         k_codes = keep.tile([P, N], U32, name="k_codes", align_bytes=64)
         k_scales = keep.tile([P, N], U8, name="k_scales", align_bytes=64)
-        qb = [keep.tile([P, P, T], BF16, name=f"qb{m}", align_bytes=64) for m in range(4)]
-        q_codes = [keep.tile([P, P], U32, name=f"q_codes{m}", align_bytes=64) for m in range(4)]
-        q_scales = [keep.tile([P, P], U8, name=f"q_scales{m}", align_bytes=64) for m in range(4)]
+        qb = [keep.tile([P, P, PLANES], BF16, name=f"qb{m}", align_bytes=64) for m in range(Q // P)]
+        q_codes = [keep.tile([P, P], U32, name=f"q_codes{m}", align_bytes=64) for m in range(Q // P)]
+        q_scales = [keep.tile([P, P], U8, name=f"q_scales{m}", align_bytes=64) for m in range(Q // P)]
 
-        def weave(copy, dst, src):
+        def interleave(copy, dst, src):
             copy(
-                out=dst.rearrange("p (c i) t -> p c t i", i=4),
-                in_=src.rearrange("p t (c i) -> p c t i", i=4),
+                out=dst.rearrange("p (c i) t -> p c t i", i=RUN),
+                in_=src.rearrange("p t (c i) -> p c t i", i=RUN),
             )
 
-        engines = {"v": nc.vector.tensor_copy, "s": nc.scalar.copy, "g": nc.gpsimd.tensor_copy}
+        def interleave_q(copy, m, a, b):
+            load, first = divmod(P * m, Q_LOAD)
+            interleave(copy, qb[m][:, a:b, :], raws[load][:, :, first + a : first + b])
 
-        def gather_half(t, h):
-            cols = slice(128 * h, 128 * h + 128)
-            nc.vector.tensor_tensor(
-                ks[:, t, cols], books[t][:].indirect(offsets[:, 8 * h : 8 * h + 8]), norm_t[:, cols], MULT)
+        def gather_scaled(t, cols):
+            entries = offsets[:, cols.start // LIST_ROWS : cols.stop // LIST_ROWS]
+            nc.vector.tensor_tensor(ks[:, t, cols], books[t][:].indirect(entries), norm_t[:, cols], MULT)
 
-        def gather(t):
-            nc.vector.tensor_tensor(ks[:, t, :], books[t][:].indirect(offsets[:]), norm_t[:], MULT)
-
-        def scalar_gather(t):
-            book16 = keep.tile([P, C], BF16, name=f"book16_{t}")
-            picked[t] = keep.tile([P, N], BF16, name=f"picked{t}")
-            nc.scalar.activation(book16[:], books[t][:], COPY)
-            nc.scalar.activation(picked[t][:], book16[:].indirect(offsets[:]), COPY)
-
-        def scale(t):
-            nc.vector.tensor_tensor(ks[:, t, :], picked[t][:], norm_t[:], MULT)
-
-        def ki(e, a, b):
-            weave(engines[e], kb[:, a:b, :], ks[:, :, a:b])
-
-        def kq(a, b):
+        def quantise(codes, scales, values):
             nc.vector.quantize_mx(
-                out=k_codes[:, a:b].bitcast(FP8X4), scales=k_scales[:, a:b],
-                in_=kb[:, a:b, :].rearrange("p c t -> p (c t)"))
+                out=codes.bitcast(FP8X4), scales=scales, in_=values.rearrange("p c t -> p (c t)")
+            )
 
-        def qi(e, m, a, b):
-            lo = 128 * m + a
-            for i, (x, y) in enumerate(q_cuts):
-                if x <= lo < y:
-                    weave(engines[e], qb[m][:, a:b, :], raws[i][:, :, lo - x : lo - x + b - a])
+        def product(m, parts):
+            quantise(q_codes[m][:], q_scales[m][:], qb[m][:])
+            banks = []
+            for cols in parts:
+                acc = psum.tile([P, cols.stop - cols.start], F32, name=f"acc{m}_{cols.start}")
+                nc.tensor.matmul_mx(
+                    out=acc[:],
+                    lhsT=q_codes[m][:].bitcast(FP8X4),
+                    lhsT_scale=q_scales[m][:],
+                    rhs=k_codes[:, cols].bitcast(FP8X4),
+                    rhs_scale=k_scales[:, cols],
+                    start=True,
+                    stop=True,
+                )
+                banks.append((cols, acc))
+            return banks
 
-        def qq(m):
-            nc.vector.quantize_mx(
-                out=q_codes[m][:].bitcast(FP8X4), scales=q_scales[m][:],
-                in_=qb[m][:].rearrange("p c t -> p (c t)"))
+        def store(m, banks, copies):
+            res = keep.tile([P, N], F32, name=f"res{m}")
+            for (cols, acc), copy in zip(banks, copies):
+                copy(out=res[:, cols], in_=acc[:])
+            nc.sync.dma_start(out[0, P * m : P * (m + 1), :], res[:])
 
-        out_rows = out[0].rearrange("(m p) n -> m p n", p=P)
-        accs = {}
-        ress = {}
+        cb_planes = cb.rearrange("(p t) c -> p t c", t=PLANES)
+        q_planes = qT[0].rearrange("(p t) q -> p t q", t=PLANES)
+        nc.sync.dma_start(norm_rows[:], norm[0 : P * BLOCK // N, :].rearrange("r (b y) -> (r b) y", y=BLOCK))
+        nc.sync.dma_start(books[0][:], cb_planes[:, 0, :])
+        nc.sync.dma_start(offsets[:], offs)
+        for t in range(1, PLANES):
+            nc.sync.dma_start(books[t][:], cb_planes[:, t, :])
+        for load, raw in enumerate(raws):
+            nc.sync.dma_start(raw[:], q_planes[:, :, Q_LOAD * load : Q_LOAD * (load + 1)])
 
-        def mm(m, a=0, b=N):
-            acc = psum.tile([P, b - a], F32, name=f"acc{m}_{a}")
-            accs[(m, a)] = acc
-            nc.tensor.matmul_mx(
-                out=acc[:],
-                lhsT=q_codes[m][:].bitcast(FP8X4), lhsT_scale=q_scales[m][:],
-                rhs=k_codes[:, a:b].bitcast(FP8X4), rhs_scale=k_scales[:, a:b],
-                start=True, stop=True)
+        nc.vector.transpose(norm_cols[:], norm_rows[:])
+        for cols in HALVES:
+            squares = slice(cols.start // BLOCK, cols.stop // BLOCK)
+            nc.vector.tensor_copy(
+                out=norm_wide[:, cols].rearrange("p (b x) -> p b x", x=BLOCK),
+                in_=norm_cols[:, squares].unsqueeze(2).to_broadcast([P, squares.stop - squares.start, BLOCK]),
+            )
+        for cols in HALVES:
+            nc.vector.transpose(norm_t[:, cols], norm_wide[:, cols])
 
-        def ev(e, m, a=0, b=N):
-            if m not in ress:
-                ress[m] = keep.tile([P, N], F32, name=f"res{m}")
-            engines[e](out=ress[m][:, a:b], in_=accs[(m, a)][:])
+        book16 = keep.tile([P, C], BF16, name="book16_1")
+        picked = keep.tile([P, N], BF16, name="picked1")
+        nc.scalar.activation(book16[:], books[SCALAR_PLANE][:], COPY)
+        nc.scalar.activation(picked[:], book16[:].indirect(offsets[:]), COPY)
+        interleave_q(nc.scalar.copy, 0, 0, P)
+        interleave_q(nc.scalar.copy, 1, 0, P)
+        interleave_q(nc.scalar.copy, 3, 0, SCALAR_SHARE)
 
-        def st(m, a=0, b=N):
-            nc.sync.dma_start(out_rows[m][:, a:b], ress[m][:, a:b])
+        for cols in HALVES:
+            gather_scaled(0, cols)
+        gather_scaled(2, slice(0, N))
+        for cols in HALVES:
+            gather_scaled(3, cols)
+        for cols in HALVES:
+            nc.vector.tensor_tensor(ks[:, SCALAR_PLANE, cols], picked[:, cols], norm_t[:, cols], MULT)
+        for cols in HALVES:
+            interleave(nc.vector.tensor_copy, kb[:, cols, :], ks[:, :, cols])
+        for cols in HALVES:
+            quantise(k_codes[:, cols], k_scales[:, cols], kb[:, cols, :])
 
-        ld_cb(0)
-        ld_norm(nc.sync)
-        ld_offs()
-        ld_cb(1)
-        ld_cb(2)
-        ld_cb(3)
-        ld_q(0)
-        ld_q(1)
-        spread_norm()
-        scalar_gather(1)
-        qi("s", 0, 0, 128)
-        qi("s", 1, 0, 128)
-        qi("s", 3, 0, 96)
-        gather_half(0, 0)
-        gather_half(0, 1)
-        gather(2)
-        scale(1)
-        gather_half(3, 0)
-        gather_half(3, 1)
-        ki("v", 0, 128)
-        ki("v", 128, 256)
-        kq(0, 128)
-        kq(128, 256)
-        qq(0)
-        mm(0)
-        qq(1)
-        mm(1)
-        qi("v", 3, 96, 128)
-        qi("v", 2, 0, 128)
-        qq(3)
-        mm(3, 0, 128)
-        mm(3, 128, 256)
-        qq(2)
-        mm(2, 0, 128)
-        mm(2, 128, 256)
-        ev("s", 0)
-        st(0)
-        ev("s", 1)
-        st(1)
-        ev("v", 3, 0, 128)
-        ev("s", 3, 128, 256)
-        st(3)
-        ev("v", 2, 0, 128)
-        ev("s", 2, 128, 256)
-        st(2)
+        banks = {m: product(m, [slice(0, N)]) for m in (0, 1)}
+        interleave_q(nc.vector.tensor_copy, 3, SCALAR_SHARE, P)
+        interleave_q(nc.vector.tensor_copy, 2, 0, P)
+        for m in (3, 2):
+            banks[m] = product(m, HALVES)
+        for m in (0, 1):
+            store(m, banks[m], [nc.scalar.copy])
+        for m in (3, 2):
+            store(m, banks[m], [nc.vector.tensor_copy, nc.scalar.copy])

@@ -18,10 +18,11 @@ PLANES = 4
 BLOCK = 32
 LIST_ROWS = 16
 RUN = 4
-HALVES = (slice(0, N // 2), slice(N // 2, N))
+HALVES = (slice(N // 2, N), slice(0, N // 2))
 Q_LOAD = Q // 2
 SCALAR_PLANE = 1
-SCALAR_SHARE = 96
+SCALAR_SHARE = 72
+VECTOR_SHARE = 64
 FLOPS = 2 * D * Q * N
 
 
@@ -38,11 +39,13 @@ def tile_attend_pq_lin_kernel(tc, qT, cb, norm, offs, out):
         books = [keep.tile([P, C], F32, name=f"book{t}") for t in range(PLANES)]
         raws = [keep.tile([P, PLANES, Q_LOAD], F32, name=f"raw{a}") for a in range(0, Q, Q_LOAD)]
 
-        ks = keep.tile([P, PLANES, N], F32, name="ks")
+        ks_row = keep.tile([P, PLANES * N + P], F32, name="ks_row", align_bytes=64)
+        ks = ks_row[:, : PLANES * N].rearrange("p (t n) -> p t n", t=PLANES)
         kb = keep.tile([P, N, PLANES], BF16, name="kb", align_bytes=64)
         k_codes = keep.tile([P, N], U32, name="k_codes", align_bytes=64)
         k_scales = keep.tile([P, N], U8, name="k_scales", align_bytes=64)
-        qb = [keep.tile([P, P, PLANES], BF16, name=f"qb{m}", align_bytes=64) for m in range(Q // P)]
+        qb = {m: keep.tile([P, P, PLANES], BF16, name=f"qb{m}", align_bytes=64)[:] for m in (0, 2, 3)}
+        qb[1] = ks_row[:, PLANES * N - P :].bitcast(BF16).rearrange("p (c t) -> p c t", t=PLANES)
         q_codes = [keep.tile([P, P], U32, name=f"q_codes{m}", align_bytes=64) for m in range(Q // P)]
         q_scales = [keep.tile([P, P], U8, name=f"q_scales{m}", align_bytes=64) for m in range(Q // P)]
 
@@ -66,7 +69,7 @@ def tile_attend_pq_lin_kernel(tc, qT, cb, norm, offs, out):
             )
 
         def product(m, parts):
-            quantise(q_codes[m][:], q_scales[m][:], qb[m][:])
+            quantise(q_codes[m][:], q_scales[m][:], qb[m])
             banks = []
             for cols in parts:
                 acc = psum.tile([P, cols.stop - cols.start], F32, name=f"acc{m}_{cols.start}")
@@ -113,7 +116,7 @@ def tile_attend_pq_lin_kernel(tc, qT, cb, norm, offs, out):
         nc.scalar.activation(book16[:], books[SCALAR_PLANE][:], COPY)
         nc.scalar.activation(picked[:], book16[:].indirect(offsets[:]), COPY)
         interleave_q(nc.scalar.copy, 0, 0, P)
-        interleave_q(nc.scalar.copy, 1, 0, P)
+        interleave_q(nc.scalar.copy, 1, VECTOR_SHARE, P)
         interleave_q(nc.scalar.copy, 3, 0, SCALAR_SHARE)
 
         for cols in HALVES:
@@ -125,8 +128,10 @@ def tile_attend_pq_lin_kernel(tc, qT, cb, norm, offs, out):
             nc.vector.tensor_tensor(ks[:, SCALAR_PLANE, cols], picked[:, cols], norm_t[:, cols], MULT)
         for cols in HALVES:
             interleave(nc.vector.tensor_copy, kb[:, cols, :], ks[:, :, cols])
-        for cols in HALVES:
-            quantise(k_codes[:, cols], k_scales[:, cols], kb[:, cols, :])
+        first, last = HALVES
+        quantise(k_codes[:, first], k_scales[:, first], kb[:, first, :])
+        interleave_q(nc.vector.tensor_copy, 1, 0, VECTOR_SHARE)
+        quantise(k_codes[:, last], k_scales[:, last], kb[:, last, :])
 
         banks = {m: product(m, [slice(0, N)]) for m in (0, 1)}
         interleave_q(nc.vector.tensor_copy, 3, SCALAR_SHARE, P)

@@ -19,10 +19,8 @@ BLOCK = 32
 LIST_ROWS = 16
 RUN = 4
 HALVES = (slice(N // 2, N), slice(0, N // 2))
-Q_LOAD = Q // 2
 SCALAR_PLANE = 1
-SCALAR_SHARE = 72
-VECTOR_SHARE = 64
+SHARE = P // 2
 FLOPS = 2 * D * Q * N
 
 
@@ -37,15 +35,16 @@ def tile_attend_pq_lin_kernel(tc, qT, cb, norm, offs, out):
         norm_cols = keep.tile([P, BLOCK], F32, name="norm_cols", align_bytes=64)
         norm_wide = keep.tile([P, N], F32, name="norm_wide", align_bytes=64)
         books = [keep.tile([P, C], F32, name=f"book{t}") for t in range(PLANES)]
-        raws = [keep.tile([P, PLANES, Q_LOAD], F32, name=f"raw{a}") for a in range(0, Q, Q_LOAD)]
+        raw = keep.tile([P, PLANES * Q], F32, name="raw")
 
-        ks_row = keep.tile([P, PLANES * N + P], F32, name="ks_row", align_bytes=64)
-        ks = ks_row[:, : PLANES * N].rearrange("p (t n) -> p t n", t=PLANES)
+        ks_row = keep.tile([P, P + PLANES * N + P], F32, name="ks_row", align_bytes=64)
+        ks = ks_row[:, P : P + PLANES * N].rearrange("p (t n) -> p t n", t=PLANES)
         kb = keep.tile([P, N, PLANES], BF16, name="kb", align_bytes=64)
         k_codes = keep.tile([P, N], U32, name="k_codes", align_bytes=64)
         k_scales = keep.tile([P, N], U8, name="k_scales", align_bytes=64)
-        qb = {m: keep.tile([P, P, PLANES], BF16, name=f"qb{m}", align_bytes=64)[:] for m in (0, 2, 3)}
-        qb[1] = ks_row[:, PLANES * N - P :].bitcast(BF16).rearrange("p (c t) -> p c t", t=PLANES)
+        qb = {m: keep.tile([P, P, PLANES], BF16, name=f"qb{m}", align_bytes=64)[:] for m in (2, 3)}
+        qb[0] = ks_row[:, PLANES * N :].bitcast(BF16).rearrange("p (c t) -> p c t", t=PLANES)
+        qb[1] = ks_row[:, : 2 * P].bitcast(BF16).rearrange("p (c t) -> p c t", t=PLANES)
         q_codes = [keep.tile([P, P], U32, name=f"q_codes{m}", align_bytes=64) for m in range(Q // P)]
         q_scales = [keep.tile([P, P], U8, name=f"q_scales{m}", align_bytes=64) for m in range(Q // P)]
 
@@ -56,8 +55,8 @@ def tile_attend_pq_lin_kernel(tc, qT, cb, norm, offs, out):
             )
 
         def interleave_q(copy, m, a, b):
-            load, first = divmod(P * m, Q_LOAD)
-            interleave(copy, qb[m][:, a:b, :], raws[load][:, :, first + a : first + b])
+            planes = raw[:].rearrange("p (t q) -> p t q", t=PLANES)
+            interleave(copy, qb[m][:, a:b, :], planes[:, :, P * m + a : P * m + b])
 
         def gather_scaled(t, cols):
             entries = offsets[:, cols.start // LIST_ROWS : cols.stop // LIST_ROWS]
@@ -92,14 +91,15 @@ def tile_attend_pq_lin_kernel(tc, qT, cb, norm, offs, out):
             nc.sync.dma_start(out[0, P * m : P * (m + 1), :], res[:])
 
         cb_planes = cb.rearrange("(p t) c -> p t c", t=PLANES)
-        q_planes = qT[0].rearrange("(p t) q -> p t q", t=PLANES)
+        q_pairs = qT[0].rearrange("(p u e) q -> p u (e q)", u=2, e=2)
+        raw_pairs = raw[:].rearrange("p (u x) -> p u x", u=2)
         nc.sync.dma_start(norm_rows[:], norm[0 : P * BLOCK // N, :].rearrange("r (b y) -> (r b) y", y=BLOCK))
         nc.sync.dma_start(books[0][:], cb_planes[:, 0, :])
         nc.sync.dma_start(offsets[:], offs)
         for t in range(1, PLANES):
             nc.sync.dma_start(books[t][:], cb_planes[:, t, :])
-        for load, raw in enumerate(raws):
-            nc.sync.dma_start(raw[:], q_planes[:, :, Q_LOAD * load : Q_LOAD * (load + 1)])
+        for part in (slice(0, Q + Q // 2), slice(Q + Q // 2, 2 * Q)):
+            nc.sync.dma_start(raw_pairs[:, :, part], q_pairs[:, :, part])
 
         nc.vector.transpose(norm_cols[:], norm_rows[:])
         for cols in HALVES:
@@ -115,9 +115,9 @@ def tile_attend_pq_lin_kernel(tc, qT, cb, norm, offs, out):
         picked = keep.tile([P, N], BF16, name="picked1")
         nc.scalar.activation(book16[:], books[SCALAR_PLANE][:], COPY)
         nc.scalar.activation(picked[:], book16[:].indirect(offsets[:]), COPY)
-        interleave_q(nc.scalar.copy, 0, 0, P)
-        interleave_q(nc.scalar.copy, 1, VECTOR_SHARE, P)
-        interleave_q(nc.scalar.copy, 3, 0, SCALAR_SHARE)
+        interleave_q(nc.scalar.copy, 0, SHARE, P)
+        interleave_q(nc.scalar.copy, 1, 0, SHARE)
+        interleave_q(nc.scalar.copy, 3, 0, P)
 
         for cols in HALVES:
             gather_scaled(0, cols)
@@ -130,11 +130,11 @@ def tile_attend_pq_lin_kernel(tc, qT, cb, norm, offs, out):
             interleave(nc.vector.tensor_copy, kb[:, cols, :], ks[:, :, cols])
         first, last = HALVES
         quantise(k_codes[:, first], k_scales[:, first], kb[:, first, :])
-        interleave_q(nc.vector.tensor_copy, 1, 0, VECTOR_SHARE)
+        interleave_q(nc.vector.tensor_copy, 0, 0, SHARE)
         quantise(k_codes[:, last], k_scales[:, last], kb[:, last, :])
+        interleave_q(nc.vector.tensor_copy, 1, SHARE, P)
 
         banks = {m: product(m, [slice(0, N)]) for m in (0, 1)}
-        interleave_q(nc.vector.tensor_copy, 3, SCALAR_SHARE, P)
         interleave_q(nc.vector.tensor_copy, 2, 0, P)
         for m in (3, 2):
             banks[m] = product(m, HALVES)

@@ -20,7 +20,7 @@ LIST_ROWS = 16
 RUN = 4
 HALVES = (slice(N // 2, N), slice(0, N // 2))
 SCALAR_PLANE = 1
-SHARE = P // 2
+VECTOR_SHARES = (0, 64, 64, 88)
 FLOPS = 2 * D * Q * N
 
 
@@ -37,14 +37,20 @@ def tile_attend_pq_lin_kernel(tc, qT, cb, norm, offs, out):
         books = [keep.tile([P, C], F32, name=f"book{t}") for t in range(PLANES)]
         raw = keep.tile([P, PLANES * Q], F32, name="raw")
 
-        ks_row = keep.tile([P, P + PLANES * N + P], F32, name="ks_row", align_bytes=64)
-        ks = ks_row[:, P : P + PLANES * N].rearrange("p (t n) -> p t n", t=PLANES)
-        kb = keep.tile([P, N, PLANES], BF16, name="kb", align_bytes=64)
+        ks_row = keep.tile([P, PLANES * N + P], F32, name="ks_row", align_bytes=64)
+        ks = ks_row[:, : PLANES * N].rearrange("p (t n) -> p t n", t=PLANES)
+        lead = P - VECTOR_SHARES[2]
+        kb_row = keep.tile([P, lead + N + P - VECTOR_SHARES[3], PLANES], BF16, name="kb_row", align_bytes=64)
+        kb = kb_row[:, lead : lead + N, :]
         k_codes = keep.tile([P, N], U32, name="k_codes", align_bytes=64)
         k_scales = keep.tile([P, N], U8, name="k_scales", align_bytes=64)
-        qb = {m: keep.tile([P, P, PLANES], BF16, name=f"qb{m}", align_bytes=64)[:] for m in (2, 3)}
-        qb[0] = ks_row[:, PLANES * N :].bitcast(BF16).rearrange("p (c t) -> p c t", t=PLANES)
-        qb[1] = ks_row[:, : 2 * P].bitcast(BF16).rearrange("p (c t) -> p c t", t=PLANES)
+        qb0 = keep.tile([P, P, PLANES], BF16, name="qb0", align_bytes=64)
+        qb = [
+            qb0[:],
+            ks_row[:, PLANES * N - P :].bitcast(BF16).rearrange("p (c t) -> p c t", t=PLANES),
+            kb_row[:, :P, :],
+            kb_row[:, lead + N - VECTOR_SHARES[3] :, :],
+        ]
         q_codes = [keep.tile([P, P], U32, name=f"q_codes{m}", align_bytes=64) for m in range(Q // P)]
         q_scales = [keep.tile([P, P], U8, name=f"q_scales{m}", align_bytes=64) for m in range(Q // P)]
 
@@ -98,7 +104,8 @@ def tile_attend_pq_lin_kernel(tc, qT, cb, norm, offs, out):
         nc.sync.dma_start(offsets[:], offs)
         for t in range(1, PLANES):
             nc.sync.dma_start(books[t][:], cb_planes[:, t, :])
-        for part in (slice(0, Q + Q // 2), slice(Q + Q // 2, 2 * Q)):
+        for m in range(Q // P):
+            part = slice(Q + P * m if m else 0, Q + P * (m + 1))
             nc.sync.dma_start(raw_pairs[:, :, part], q_pairs[:, :, part])
 
         nc.vector.transpose(norm_cols[:], norm_rows[:])
@@ -115,9 +122,10 @@ def tile_attend_pq_lin_kernel(tc, qT, cb, norm, offs, out):
         picked = keep.tile([P, N], BF16, name="picked1")
         nc.scalar.activation(book16[:], books[SCALAR_PLANE][:], COPY)
         nc.scalar.activation(picked[:], book16[:].indirect(offsets[:]), COPY)
-        interleave_q(nc.scalar.copy, 0, SHARE, P)
-        interleave_q(nc.scalar.copy, 1, 0, SHARE)
-        interleave_q(nc.scalar.copy, 3, 0, P)
+        interleave_q(nc.scalar.copy, 0, 0, P)
+        interleave_q(nc.scalar.copy, 1, VECTOR_SHARES[1], P)
+        interleave_q(nc.scalar.copy, 2, 0, P - VECTOR_SHARES[2])
+        interleave_q(nc.scalar.copy, 3, VECTOR_SHARES[3], P)
 
         for cols in HALVES:
             gather_scaled(0, cols)
@@ -130,15 +138,16 @@ def tile_attend_pq_lin_kernel(tc, qT, cb, norm, offs, out):
             interleave(nc.vector.tensor_copy, kb[:, cols, :], ks[:, :, cols])
         first, last = HALVES
         quantise(k_codes[:, first], k_scales[:, first], kb[:, first, :])
-        interleave_q(nc.vector.tensor_copy, 0, 0, SHARE)
+        interleave_q(nc.vector.tensor_copy, 1, 0, VECTOR_SHARES[1])
         quantise(k_codes[:, last], k_scales[:, last], kb[:, last, :])
-        interleave_q(nc.vector.tensor_copy, 1, SHARE, P)
 
-        banks = {m: product(m, [slice(0, N)]) for m in (0, 1)}
-        interleave_q(nc.vector.tensor_copy, 2, 0, P)
-        for m in (3, 2):
+        banks = {0: product(0, HALVES)}
+        interleave_q(nc.vector.tensor_copy, 2, P - VECTOR_SHARES[2], P)
+        banks[1] = product(1, [slice(0, N)])
+        interleave_q(nc.vector.tensor_copy, 3, 0, VECTOR_SHARES[3])
+        for m in (2, 3):
             banks[m] = product(m, HALVES)
         for m in (0, 1):
-            store(m, banks[m], [nc.scalar.copy])
-        for m in (3, 2):
+            store(m, banks[m], [nc.scalar.copy, nc.scalar.copy])
+        for m in (2, 3):
             store(m, banks[m], [nc.vector.tensor_copy, nc.scalar.copy])

@@ -20,7 +20,7 @@ LIST_ROWS = 16
 RUN = 4
 HALVES = (slice(N // 2, N), slice(0, N // 2))
 SCALAR_PLANE = 1
-VECTOR_SHARES = (0, 64, 64, 88)
+VECTOR_SHARES = (32, 32, 64, 88)
 FLOPS = 2 * D * Q * N
 
 
@@ -37,17 +37,18 @@ def tile_attend_pq_lin_kernel(tc, qT, cb, norm, offs, out):
         books = [keep.tile([P, C], F32, name=f"book{t}") for t in range(PLANES)]
         raw = keep.tile([P, PLANES * Q], F32, name="raw")
 
-        ks_row = keep.tile([P, PLANES * N + P], F32, name="ks_row", align_bytes=64)
+        ks_row = keep.tile([P, PLANES * N + 2 * (P - VECTOR_SHARES[1])], F32, name="ks_row", align_bytes=64)
         ks = ks_row[:, : PLANES * N].rearrange("p (t n) -> p t n", t=PLANES)
         lead = P - VECTOR_SHARES[2]
         kb_row = keep.tile([P, lead + N + P - VECTOR_SHARES[3], PLANES], BF16, name="kb_row", align_bytes=64)
         kb = kb_row[:, lead : lead + N, :]
         k_codes = keep.tile([P, N], U32, name="k_codes", align_bytes=64)
         k_scales = keep.tile([P, N], U8, name="k_scales", align_bytes=64)
-        qb0 = keep.tile([P, P, PLANES], BF16, name="qb0", align_bytes=64)
+        picked_row = keep.tile([P, N + PLANES * (P - VECTOR_SHARES[0])], BF16, name="picked_row", align_bytes=64)
+        picked = picked_row[:, :N]
         qb = [
-            qb0[:],
-            ks_row[:, PLANES * N - P :].bitcast(BF16).rearrange("p (c t) -> p c t", t=PLANES),
+            picked_row[:, N - PLANES * VECTOR_SHARES[0] :].rearrange("p (c t) -> p c t", t=PLANES),
+            ks_row[:, PLANES * N - 2 * VECTOR_SHARES[1] :].bitcast(BF16).rearrange("p (c t) -> p c t", t=PLANES),
             kb_row[:, :P, :],
             kb_row[:, lead + N - VECTOR_SHARES[3] :, :],
         ]
@@ -119,10 +120,9 @@ def tile_attend_pq_lin_kernel(tc, qT, cb, norm, offs, out):
             nc.vector.transpose(norm_t[:, cols], norm_wide[:, cols])
 
         book16 = keep.tile([P, C], BF16, name="book16_1")
-        picked = keep.tile([P, N], BF16, name="picked1")
         nc.scalar.activation(book16[:], books[SCALAR_PLANE][:], COPY)
-        nc.scalar.activation(picked[:], book16[:].indirect(offsets[:]), COPY)
-        interleave_q(nc.scalar.copy, 0, 0, P)
+        nc.scalar.activation(picked, book16[:].indirect(offsets[:]), COPY)
+        interleave_q(nc.scalar.copy, 0, VECTOR_SHARES[0], P)
         interleave_q(nc.scalar.copy, 1, VECTOR_SHARES[1], P)
         interleave_q(nc.scalar.copy, 2, 0, P - VECTOR_SHARES[2])
         interleave_q(nc.scalar.copy, 3, VECTOR_SHARES[3], P)
@@ -137,6 +137,7 @@ def tile_attend_pq_lin_kernel(tc, qT, cb, norm, offs, out):
         for cols in HALVES:
             interleave(nc.vector.tensor_copy, kb[:, cols, :], ks[:, :, cols])
         first, last = HALVES
+        interleave_q(nc.vector.tensor_copy, 0, 0, VECTOR_SHARES[0])
         quantise(k_codes[:, first], k_scales[:, first], kb[:, first, :])
         interleave_q(nc.vector.tensor_copy, 1, 0, VECTOR_SHARES[1])
         quantise(k_codes[:, last], k_scales[:, last], kb[:, last, :])

@@ -144,7 +144,7 @@ def tile_attend_pq_lin_kernel(tc, qT, cb, norm, offs, out):
 
         banks = {0: product(0, HALVES)}
         interleave_q(nc.vector.tensor_copy, 2, P - VECTOR_SHARES[2], P)
-        banks[1] = product(1, [slice(0, N)])
+        banks[1] = product(1, HALVES)
         interleave_q(nc.vector.tensor_copy, 3, 0, VECTOR_SHARES[3])
         for m in (2, 3):
             banks[m] = product(m, HALVES)

@@ -20,7 +20,7 @@ LIST_ROWS = 16
 RUN = 4
 HALVES = (slice(N // 2, N), slice(0, N // 2))
 SCALAR_PLANE = 1
-VECTOR_SHARES = (32, 32, 64, 88)
+VECTOR_SHARES = (32, 32, 48, 64)
 FLOPS = 2 * D * Q * N
 
 
@@ -129,9 +129,8 @@ def tile_attend_pq_lin_kernel(tc, qT, cb, norm, offs, out):
 
         for cols in HALVES:
             gather_scaled(0, cols)
-        gather_scaled(2, slice(0, N))
-        for cols in HALVES:
-            gather_scaled(3, cols)
+        for t in (2, 3):
+            gather_scaled(t, slice(0, N))
         for cols in HALVES:
             nc.vector.tensor_tensor(ks[:, SCALAR_PLANE, cols], picked[:, cols], norm_t[:, cols], MULT)
         for cols in HALVES:

@@ -20,7 +20,7 @@ LIST_ROWS = 16
 RUN = 4
 HALVES = (slice(N // 2, N), slice(0, N // 2))
 SCALAR_PLANE = 1
-VECTOR_SHARES = (32, 32, 48, 64)
+VECTOR_SHARES = (32, 32, 80, 104)
 FLOPS = 2 * D * Q * N
 
 

@@ -20,7 +20,7 @@ LIST_ROWS = 16
 RUN = 4
 HALVES = (slice(N // 2, N), slice(0, N // 2))
 SCALAR_PLANE = 1
-VECTOR_SHARES = (32, 32, 80, 104)
+VECTOR_SHARES = (32, 32, 80, 72)
 FLOPS = 2 * D * Q * N
 
 
@@ -144,9 +144,9 @@ def tile_attend_pq_lin_kernel(tc, qT, cb, norm, offs, out):
         banks = {0: product(0, HALVES)}
         interleave_q(nc.vector.tensor_copy, 2, P - VECTOR_SHARES[2], P)
         banks[1] = product(1, HALVES)
+        banks[2] = product(2, HALVES)
         interleave_q(nc.vector.tensor_copy, 3, 0, VECTOR_SHARES[3])
-        for m in (2, 3):
-            banks[m] = product(m, HALVES)
+        banks[3] = product(3, HALVES)
         for m in (0, 1):
             store(m, banks[m], [nc.scalar.copy, nc.scalar.copy])
         for m in (2, 3):

@@ -20,7 +20,7 @@ LIST_ROWS = 16
 RUN = 4
 HALVES = (slice(N // 2, N), slice(0, N // 2))
 SCALAR_PLANE = 1
-VECTOR_SHARES = (32, 32, 80, 72)
+VECTOR_SHARES = (48, 32, 64, 72)
 FLOPS = 2 * D * Q * N
 
 

@@ -18,9 +18,11 @@ PLANES = 4
 BLOCK = 32
 LIST_ROWS = 16
 RUN = 4
-HALVES = (slice(N // 2, N), slice(0, N // 2))
-SCALAR_PLANE = 1
-VECTOR_SHARES = (48, 32, 64, 72)
+HALF = N // 2
+FUSED, PLAIN = slice(0, HALF), slice(HALF, N)
+VECTOR_SHARES = (56, 40, 48, 72)
+EDGE = 8
+K_SHARE = 32
 FLOPS = 2 * D * Q * N
 
 
@@ -29,55 +31,51 @@ def tile_attend_pq_lin_kernel(tc, qT, cb, norm, offs, out):
     with ExitStack() as ctx:
         keep = ctx.enter_context(tc.tile_pool(name="keep", bufs=1))
         psum = ctx.enter_context(tc.psum_pool(name="psum", bufs=1))
-        offsets = keep.tile([P, N // LIST_ROWS], U16, name="offsets")
-        norm_t = keep.tile([P, N], F32, name="norm_t", align_bytes=64)
-        norm_rows = keep.tile([P, BLOCK], F32, name="norm_rows", align_bytes=64)
-        norm_cols = keep.tile([P, BLOCK], F32, name="norm_cols", align_bytes=64)
-        norm_wide = keep.tile([P, N], F32, name="norm_wide", align_bytes=64)
-        books = [keep.tile([P, C], F32, name=f"book{t}") for t in range(PLANES)]
-        raw = keep.tile([P, PLANES * Q], F32, name="raw")
+        offsets = keep.tile([P, N // LIST_ROWS], U16, name="offsets", align_bytes=256)
+        norm_rows = keep.tile([P, BLOCK], F32, name="norm_rows", align_bytes=256)
+        norm_cols = keep.tile([P, BLOCK], F32, name="norm_cols", align_bytes=256)
+        norm_wide = keep.tile([P, N], F32, name="norm_wide", align_bytes=256)
+        norm_t = keep.tile([P, N], F32, name="norm_t", align_bytes=256)
+        books = [keep.tile([P, C], F32, name=f"book{t}", align_bytes=256) for t in range(PLANES)]
+        raw = keep.tile([P, PLANES * Q], F32, name="raw", align_bytes=256)
+        book16 = keep.tile([P, C], BF16, name="book16", align_bytes=256)
+        scaled = keep.tile([P, PLANES * HALF], F32, name="scaled")[:].rearrange("p (t n) -> p t n", t=PLANES)
 
-        ks_row = keep.tile([P, PLANES * N + 2 * (P - VECTOR_SHARES[1])], F32, name="ks_row", align_bytes=64)
-        ks = ks_row[:, : PLANES * N].rearrange("p (t n) -> p t n", t=PLANES)
-        lead = P - VECTOR_SHARES[2]
-        kb_row = keep.tile([P, lead + N + P - VECTOR_SHARES[3], PLANES], BF16, name="kb_row", align_bytes=64)
-        kb = kb_row[:, lead : lead + N, :]
-        k_codes = keep.tile([P, N], U32, name="k_codes", align_bytes=64)
-        k_scales = keep.tile([P, N], U8, name="k_scales", align_bytes=64)
-        picked_row = keep.tile([P, N + PLANES * (P - VECTOR_SHARES[0])], BF16, name="picked_row", align_bytes=64)
-        picked = picked_row[:, :N]
-        qb = [
-            picked_row[:, N - PLANES * VECTOR_SHARES[0] :].rearrange("p (c t) -> p c t", t=PLANES),
-            ks_row[:, PLANES * N - 2 * VECTOR_SHARES[1] :].bitcast(BF16).rearrange("p (c t) -> p c t", t=PLANES),
-            kb_row[:, :P, :],
-            kb_row[:, lead + N - VECTOR_SHARES[3] :, :],
-        ]
-        q_codes = [keep.tile([P, P], U32, name=f"q_codes{m}", align_bytes=64) for m in range(Q // P)]
-        q_scales = [keep.tile([P, P], U8, name=f"q_scales{m}", align_bytes=64) for m in range(Q // P)]
+        def row_over(name, share):
+            row = keep.tile([P, PLANES * (HALF + P - share)], BF16, name=name, align_bytes=256)
+            return row[:, : PLANES * HALF], row[:, PLANES * (HALF - share) :].rearrange("p (c t) -> p c t", t=PLANES)
 
-        def interleave(copy, dst, src):
-            copy(
-                out=dst.rearrange("p (c i) t -> p c t i", i=RUN),
-                in_=src.rearrange("p t (c i) -> p c t i", i=RUN),
-            )
+        plain, q1 = row_over("plain_row", VECTOR_SHARES[1])
+        fused_row = keep.tile([P, PLANES * (HALF + 2 * P - VECTOR_SHARES[2])], BF16, name="fused_row", align_bytes=256)
+        k_fused = fused_row[:, : PLANES * HALF]
+        q23 = fused_row[:, PLANES * (HALF - VECTOR_SHARES[2]) :].rearrange("p (c t) -> p c t", t=PLANES)
+        k_plain = keep.tile([P, PLANES * HALF], BF16, name="k_plain", align_bytes=256)[:]
+        plain = plain.rearrange("p (t n) -> p t n", t=PLANES)
+        k_codes = keep.tile([P, N], U32, name="k_codes", align_bytes=256)
+        k_scales = keep.tile([P, N], U8, name="k_scales", align_bytes=256)
+        q_codes = [keep.tile([P, P], U32, name=f"q_codes{m}", align_bytes=256) for m in range(Q // P)]
+        q_scales = [keep.tile([P, P], U8, name=f"q_scales{m}", align_bytes=256) for m in range(Q // P)]
+
+        def runs(planes):
+            return planes.rearrange("p t (c i) -> p c t i", i=RUN)
+
+        def words(values):
+            return values.rearrange("p (c i) t -> p c t i", i=RUN)
 
         def interleave_q(copy, m, a, b):
             planes = raw[:].rearrange("p (t q) -> p t q", t=PLANES)
-            interleave(copy, qb[m][:, a:b, :], planes[:, :, P * m + a : P * m + b])
+            copy(out=words(qb[m][:, a:b, :]), in_=runs(planes[:, :, P * m + a : P * m + b]))
 
-        def gather_scaled(t, cols):
-            entries = offsets[:, cols.start // LIST_ROWS : cols.stop // LIST_ROWS]
-            nc.vector.tensor_tensor(ks[:, t, cols], books[t][:].indirect(entries), norm_t[:, cols], MULT)
+        def entries(cols):
+            return offsets[:, cols.start // LIST_ROWS : cols.stop // LIST_ROWS]
 
         def quantise(codes, scales, values):
-            nc.vector.quantize_mx(
-                out=codes.bitcast(FP8X4), scales=scales, in_=values.rearrange("p c t -> p (c t)")
-            )
+            nc.vector.quantize_mx(out=codes.bitcast(FP8X4), scales=scales, in_=values)
 
-        def product(m, parts):
-            quantise(q_codes[m][:], q_scales[m][:], qb[m])
+        def product(m):
+            quantise(q_codes[m][:], q_scales[m][:], qb[m].rearrange("p c t -> p (c t)"))
             banks = []
-            for cols in parts:
+            for cols in (FUSED, PLAIN) if m >= 2 else (slice(0, N),):
                 acc = psum.tile([P, cols.stop - cols.start], F32, name=f"acc{m}_{cols.start}")
                 nc.tensor.matmul_mx(
                     out=acc[:],
@@ -91,11 +89,12 @@ def tile_attend_pq_lin_kernel(tc, qT, cb, norm, offs, out):
                 banks.append((cols, acc))
             return banks
 
-        def store(m, banks, copies):
-            res = keep.tile([P, N], F32, name=f"res{m}")
-            for (cols, acc), copy in zip(banks, copies):
-                copy(out=res[:, cols], in_=acc[:])
-            nc.sync.dma_start(out[0, P * m : P * (m + 1), :], res[:])
+        res = [raw[:, Q * m + P : Q * m + 3 * P] for m in range(2)]
+        res += [keep.tile([P, N], F32, name=f"res{m}", align_bytes=256)[:] for m in (2, 3)]
+
+        def empty(copy, m, half):
+            cols, acc = banks[m][half]
+            copy(out=res[m][:, cols], in_=acc[:])
 
         cb_planes = cb.rearrange("(p t) c -> p t c", t=PLANES)
         q_pairs = qT[0].rearrange("(p u e) q -> p u (e q)", u=2, e=2)
@@ -110,44 +109,51 @@ def tile_attend_pq_lin_kernel(tc, qT, cb, norm, offs, out):
             nc.sync.dma_start(raw_pairs[:, :, part], q_pairs[:, :, part])
 
         nc.vector.transpose(norm_cols[:], norm_rows[:])
-        for cols in HALVES:
+        for cols in (FUSED, PLAIN):
             squares = slice(cols.start // BLOCK, cols.stop // BLOCK)
             nc.vector.tensor_copy(
                 out=norm_wide[:, cols].rearrange("p (b x) -> p b x", x=BLOCK),
-                in_=norm_cols[:, squares].unsqueeze(2).to_broadcast([P, squares.stop - squares.start, BLOCK]),
+                in_=norm_cols[:, squares].unsqueeze(2).to_broadcast([P, HALF // BLOCK, BLOCK]),
             )
-        for cols in HALVES:
+        for cols in (FUSED, PLAIN):
             nc.vector.transpose(norm_t[:, cols], norm_wide[:, cols])
 
-        book16 = keep.tile([P, C], BF16, name="book16_1")
-        nc.scalar.activation(book16[:], books[SCALAR_PLANE][:], COPY)
-        nc.scalar.activation(picked, book16[:].indirect(offsets[:]), COPY)
-        interleave_q(nc.scalar.copy, 0, VECTOR_SHARES[0], P)
-        interleave_q(nc.scalar.copy, 1, VECTOR_SHARES[1], P)
-        interleave_q(nc.scalar.copy, 2, 0, P - VECTOR_SHARES[2])
-        interleave_q(nc.scalar.copy, 3, VECTOR_SHARES[3], P)
+        nc.scalar.activation(book16[:], books[1][:], COPY)
+        for t, window in ((2, books[2]), (3, books[3]), (1, book16)):
+            nc.scalar.activation(plain[:, t, :], window[:].indirect(entries(PLAIN)), COPY)
+        nc.vector.tensor_copy(plain[:, 0, :], books[0][:].indirect(entries(PLAIN)))
+        for t in range(PLANES):
+            nc.vector.tensor_tensor(scaled[:, t, :], books[t][:].indirect(entries(FUSED)), norm_t[:, FUSED], MULT)
+        for copy, cols in ((nc.scalar.copy, slice(K_SHARE, HALF)), (nc.vector.tensor_copy, slice(0, K_SHARE))):
+            copy(out=words(k_fused.rearrange("p (c t) -> p c t", t=PLANES)[:, cols, :]), in_=runs(scaled[:, :, cols]))
+        spread = norm_t[:, PLAIN].rearrange("p (c i) -> p c i", i=RUN).unsqueeze(2)
+        nc.vector.tensor_tensor(
+            words(k_plain.rearrange("p (c t) -> p c t", t=PLANES)),
+            runs(plain),
+            spread.to_broadcast([P, HALF // RUN, PLANES, RUN]),
+            MULT,
+        )
 
-        for cols in HALVES:
-            gather_scaled(0, cols)
-        for t in (2, 3):
-            gather_scaled(t, slice(0, N))
-        for cols in HALVES:
-            nc.vector.tensor_tensor(ks[:, SCALAR_PLANE, cols], picked[:, cols], norm_t[:, cols], MULT)
-        for cols in HALVES:
-            interleave(nc.vector.tensor_copy, kb[:, cols, :], ks[:, :, cols])
-        first, last = HALVES
+        q0 = keep.tile([P, P, PLANES], BF16, name="q0", tag="book16", align_bytes=256)
+        qb = [q0[:], q1, q23[:, :P, :], q23[:, P:, :]]
+        for m in range(2):
+            interleave_q(nc.scalar.copy, m, VECTOR_SHARES[m], P)
+        interleave_q(nc.scalar.copy, 2, VECTOR_SHARES[2], P - EDGE)
+        border = raw[:].rearrange("p (t q) -> p t q", t=PLANES)[:, :, 3 * P - EDGE : 3 * P + EDGE]
+        nc.scalar.copy(out=words(q23[:, P - EDGE : P + EDGE, :]), in_=runs(border))
+        interleave_q(nc.scalar.copy, 3, EDGE, P - VECTOR_SHARES[3])
         interleave_q(nc.vector.tensor_copy, 0, 0, VECTOR_SHARES[0])
-        quantise(k_codes[:, first], k_scales[:, first], kb[:, first, :])
+        quantise(k_codes[:, FUSED], k_scales[:, FUSED], k_fused)
         interleave_q(nc.vector.tensor_copy, 1, 0, VECTOR_SHARES[1])
-        quantise(k_codes[:, last], k_scales[:, last], kb[:, last, :])
-
-        banks = {0: product(0, HALVES)}
-        interleave_q(nc.vector.tensor_copy, 2, P - VECTOR_SHARES[2], P)
-        banks[1] = product(1, HALVES)
-        banks[2] = product(2, HALVES)
-        interleave_q(nc.vector.tensor_copy, 3, 0, VECTOR_SHARES[3])
-        banks[3] = product(3, HALVES)
-        for m in (0, 1):
-            store(m, banks[m], [nc.scalar.copy, nc.scalar.copy])
-        for m in (2, 3):
-            store(m, banks[m], [nc.vector.tensor_copy, nc.scalar.copy])
+        quantise(k_codes[:, PLAIN], k_scales[:, PLAIN], k_plain)
+        banks = {0: product(0)}
+        interleave_q(nc.vector.tensor_copy, 2, 0, VECTOR_SHARES[2])
+        banks[1] = product(1)
+        interleave_q(nc.vector.tensor_copy, 3, P - VECTOR_SHARES[3], P)
+        banks[2] = product(2)
+        banks[3] = product(3)
+        for m in range(Q // P):
+            empty(nc.scalar.copy if m < 2 else nc.vector.tensor_copy, m, 0)
+            if m >= 2:
+                empty(nc.scalar.copy, m, 1)
+            nc.sync.dma_start(out[0, P * m : P * (m + 1), :], res[m])

@@ -19,10 +19,11 @@ BLOCK = 32
 LIST_ROWS = 16
 RUN = 4
 HALF = N // 2
+TILES = Q // P
 FUSED, PLAIN = slice(0, HALF), slice(HALF, N)
-VECTOR_SHARES = (56, 40, 48, 72)
-EDGE = 8
-K_SHARE = 32
+VECTOR_SHARES = (32, 56, 48, 72)
+EDGE = 4
+BORDERS = (2, 3)
 FLOPS = 2 * D * Q * N
 
 
@@ -31,40 +32,39 @@ def tile_attend_pq_lin_kernel(tc, qT, cb, norm, offs, out):
     with ExitStack() as ctx:
         keep = ctx.enter_context(tc.tile_pool(name="keep", bufs=1))
         psum = ctx.enter_context(tc.psum_pool(name="psum", bufs=1))
-        offsets = keep.tile([P, N // LIST_ROWS], U16, name="offsets", align_bytes=256)
-        norm_rows = keep.tile([P, BLOCK], F32, name="norm_rows", align_bytes=256)
-        norm_cols = keep.tile([P, BLOCK], F32, name="norm_cols", align_bytes=256)
-        norm_wide = keep.tile([P, N], F32, name="norm_wide", align_bytes=256)
-        norm_t = keep.tile([P, N], F32, name="norm_t", align_bytes=256)
-        books = [keep.tile([P, C], F32, name=f"book{t}", align_bytes=256) for t in range(PLANES)]
-        raw = keep.tile([P, PLANES * Q], F32, name="raw", align_bytes=256)
-        book16 = keep.tile([P, C], BF16, name="book16", align_bytes=256)
-        scaled = keep.tile([P, PLANES * HALF], F32, name="scaled")[:].rearrange("p (t n) -> p t n", t=PLANES)
 
-        def row_over(name, share):
-            row = keep.tile([P, PLANES * (HALF + P - share)], BF16, name=name, align_bytes=256)
-            return row[:, : PLANES * HALF], row[:, PLANES * (HALF - share) :].rearrange("p (c t) -> p c t", t=PLANES)
+        def tile(name, cols, dtype):
+            return keep.tile([P, cols], dtype, name=name, align_bytes=256)
 
-        plain, q1 = row_over("plain_row", VECTOR_SHARES[1])
-        fused_row = keep.tile([P, PLANES * (HALF + 2 * P - VECTOR_SHARES[2])], BF16, name="fused_row", align_bytes=256)
-        k_fused = fused_row[:, : PLANES * HALF]
-        q23 = fused_row[:, PLANES * (HALF - VECTOR_SHARES[2]) :].rearrange("p (c t) -> p c t", t=PLANES)
-        k_plain = keep.tile([P, PLANES * HALF], BF16, name="k_plain", align_bytes=256)[:]
-        plain = plain.rearrange("p (t n) -> p t n", t=PLANES)
-        k_codes = keep.tile([P, N], U32, name="k_codes", align_bytes=256)
-        k_scales = keep.tile([P, N], U8, name="k_scales", align_bytes=256)
-        q_codes = [keep.tile([P, P], U32, name=f"q_codes{m}", align_bytes=256) for m in range(Q // P)]
-        q_scales = [keep.tile([P, P], U8, name=f"q_scales{m}", align_bytes=256) for m in range(Q // P)]
+        offsets = tile("offsets", N // LIST_ROWS, U16)
+        norm_rows = tile("norm_rows", BLOCK, F32)
+        norm_cols = tile("norm_cols", BLOCK, F32)
+        norm_wide = {h: tile(f"norm_wide{h}", HALF, F32) for h in range(2)}
+        norm_t = {h: tile(f"norm_t{h}", HALF, F32) for h in range(2)}
+        books = [tile(f"book{t}", C, F32) for t in range(PLANES)]
+        raw = tile("raw", PLANES * Q, F32)
+        scaled = tile("scaled", PLANES * HALF, F32)[:].rearrange("p (t n) -> p t n", t=PLANES)
+        plain = tile("plain", PLANES * HALF, BF16)[:].rearrange("p (t n) -> p t n", t=PLANES)
+        early = tile("early", HALF, F32)
+        k_fused = tile("k_fused", PLANES * HALF, BF16)[:]
+        k_plain = tile("k_plain", PLANES * HALF, BF16)[:]
+        q_rows = tile("q_rows", PLANES * Q, BF16)[:]
+        k_codes = tile("k_codes", N, U32)
+        k_scales = tile("k_scales", N, U8)
+        q_codes = [tile(f"q_codes{m}", P, U32) for m in range(TILES)]
+        q_scales = [tile(f"q_scales{m}", P, U8) for m in range(TILES)]
+        res = [raw[:, Q * m + P : Q * m + 3 * P] for m in range(2)]
+        res += [tile(f"res{m}", N, F32)[:] for m in (2, 3)]
 
         def runs(planes):
             return planes.rearrange("p t (c i) -> p c t i", i=RUN)
 
         def words(values):
-            return values.rearrange("p (c i) t -> p c t i", i=RUN)
+            return values.rearrange("p (c i t) -> p c t i", i=RUN, t=PLANES)
 
-        def interleave_q(copy, m, a, b):
+        def interleave_q(copy, a, b):
             planes = raw[:].rearrange("p (t q) -> p t q", t=PLANES)
-            copy(out=words(qb[m][:, a:b, :]), in_=runs(planes[:, :, P * m + a : P * m + b]))
+            copy(out=words(q_rows[:, PLANES * a : PLANES * b]), in_=runs(planes[:, :, a:b]))
 
         def entries(cols):
             return offsets[:, cols.start // LIST_ROWS : cols.stop // LIST_ROWS]
@@ -73,7 +73,7 @@ def tile_attend_pq_lin_kernel(tc, qT, cb, norm, offs, out):
             nc.vector.quantize_mx(out=codes.bitcast(FP8X4), scales=scales, in_=values)
 
         def product(m):
-            quantise(q_codes[m][:], q_scales[m][:], qb[m].rearrange("p c t -> p (c t)"))
+            quantise(q_codes[m][:], q_scales[m][:], q_rows[:, PLANES * P * m : PLANES * P * (m + 1)])
             banks = []
             for cols in (FUSED, PLAIN) if m >= 2 else (slice(0, N),):
                 acc = psum.tile([P, cols.stop - cols.start], F32, name=f"acc{m}_{cols.start}")
@@ -89,12 +89,28 @@ def tile_attend_pq_lin_kernel(tc, qT, cb, norm, offs, out):
                 banks.append((cols, acc))
             return banks
 
-        res = [raw[:, Q * m + P : Q * m + 3 * P] for m in range(2)]
-        res += [keep.tile([P, N], F32, name=f"res{m}", align_bytes=256)[:] for m in (2, 3)]
-
         def empty(copy, m, half):
             cols, acc = banks[m][half]
             copy(out=res[m][:, cols], in_=acc[:])
+
+        def store(m):
+            nc.sync.dma_start(out[0, P * m : P * (m + 1), :], res[m])
+
+        def scalar_share(m):
+            lo = P * m
+            if m in BORDERS:
+                interleave_q(nc.scalar.copy, lo - EDGE, lo + EDGE)
+                lo = lo + EDGE
+            interleave_q(nc.scalar.copy, lo, cut(m))
+
+        def end(m):
+            return P * (m + 1) - (EDGE if m + 1 in BORDERS else 0)
+
+        def cut(m):
+            return end(m) - VECTOR_SHARES[m]
+
+        def vector_share(m):
+            interleave_q(nc.vector.tensor_copy, cut(m), end(m))
 
         cb_planes = cb.rearrange("(p t) c -> p t c", t=PLANES)
         q_pairs = qT[0].rearrange("(p u e) q -> p u (e q)", u=2, e=2)
@@ -104,56 +120,44 @@ def tile_attend_pq_lin_kernel(tc, qT, cb, norm, offs, out):
         nc.sync.dma_start(offsets[:], offs)
         for t in range(1, PLANES):
             nc.sync.dma_start(books[t][:], cb_planes[:, t, :])
-        for m in range(Q // P):
+        for m in range(TILES):
             part = slice(Q + P * m if m else 0, Q + P * (m + 1))
             nc.sync.dma_start(raw_pairs[:, :, part], q_pairs[:, :, part])
 
         nc.vector.transpose(norm_cols[:], norm_rows[:])
-        for cols in (FUSED, PLAIN):
-            squares = slice(cols.start // BLOCK, cols.stop // BLOCK)
-            nc.vector.tensor_copy(
-                out=norm_wide[:, cols].rearrange("p (b x) -> p b x", x=BLOCK),
+        for h, copy in ((0, nc.vector.tensor_copy), (1, nc.vector.tensor_copy)):
+            squares = slice(h * HALF // BLOCK, (h + 1) * HALF // BLOCK)
+            copy(
+                out=norm_wide[h][:].rearrange("p (b x) -> p b x", x=BLOCK),
                 in_=norm_cols[:, squares].unsqueeze(2).to_broadcast([P, HALF // BLOCK, BLOCK]),
             )
-        for cols in (FUSED, PLAIN):
-            nc.vector.transpose(norm_t[:, cols], norm_wide[:, cols])
+        for h in range(2):
+            nc.vector.transpose(norm_t[h][:], norm_wide[h][:])
 
-        nc.scalar.activation(book16[:], books[1][:], COPY)
-        for t, window in ((2, books[2]), (3, books[3]), (1, book16)):
-            nc.scalar.activation(plain[:, t, :], window[:].indirect(entries(PLAIN)), COPY)
-        nc.vector.tensor_copy(plain[:, 0, :], books[0][:].indirect(entries(PLAIN)))
+        nc.vector.tensor_copy(early[:], books[0][:].indirect(entries(PLAIN)))
+        nc.scalar.copy(out=plain[:, 0, :], in_=early[:])
         for t in range(PLANES):
-            nc.vector.tensor_tensor(scaled[:, t, :], books[t][:].indirect(entries(FUSED)), norm_t[:, FUSED], MULT)
-        for copy, cols in ((nc.scalar.copy, slice(K_SHARE, HALF)), (nc.vector.tensor_copy, slice(0, K_SHARE))):
-            copy(out=words(k_fused.rearrange("p (c t) -> p c t", t=PLANES)[:, cols, :]), in_=runs(scaled[:, :, cols]))
-        spread = norm_t[:, PLAIN].rearrange("p (c i) -> p c i", i=RUN).unsqueeze(2)
+            if t:
+                nc.scalar.activation(plain[:, t, :], books[t][:].indirect(entries(PLAIN)), COPY)
+            nc.vector.tensor_tensor(scaled[:, t, :], books[t][:].indirect(entries(FUSED)), norm_t[0][:], MULT)
+        nc.scalar.copy(out=words(k_fused), in_=runs(scaled))
+        spread = norm_t[1][:].rearrange("p (c i) -> p c i", i=RUN).unsqueeze(2)
         nc.vector.tensor_tensor(
-            words(k_plain.rearrange("p (c t) -> p c t", t=PLANES)),
-            runs(plain),
-            spread.to_broadcast([P, HALF // RUN, PLANES, RUN]),
-            MULT,
+            words(k_plain), runs(plain), spread.to_broadcast([P, HALF // RUN, PLANES, RUN]), MULT
         )
 
-        q0 = keep.tile([P, P, PLANES], BF16, name="q0", tag="book16", align_bytes=256)
-        qb = [q0[:], q1, q23[:, :P, :], q23[:, P:, :]]
-        for m in range(2):
-            interleave_q(nc.scalar.copy, m, VECTOR_SHARES[m], P)
-        interleave_q(nc.scalar.copy, 2, VECTOR_SHARES[2], P - EDGE)
-        border = raw[:].rearrange("p (t q) -> p t q", t=PLANES)[:, :, 3 * P - EDGE : 3 * P + EDGE]
-        nc.scalar.copy(out=words(q23[:, P - EDGE : P + EDGE, :]), in_=runs(border))
-        interleave_q(nc.scalar.copy, 3, EDGE, P - VECTOR_SHARES[3])
-        interleave_q(nc.vector.tensor_copy, 0, 0, VECTOR_SHARES[0])
-        quantise(k_codes[:, FUSED], k_scales[:, FUSED], k_fused)
-        interleave_q(nc.vector.tensor_copy, 1, 0, VECTOR_SHARES[1])
-        quantise(k_codes[:, PLAIN], k_scales[:, PLAIN], k_plain)
-        banks = {0: product(0)}
-        interleave_q(nc.vector.tensor_copy, 2, 0, VECTOR_SHARES[2])
-        banks[1] = product(1)
-        interleave_q(nc.vector.tensor_copy, 3, P - VECTOR_SHARES[3], P)
-        banks[2] = product(2)
-        banks[3] = product(3)
-        for m in range(Q // P):
+        banks = {}
+        for m in range(TILES):
+            scalar_share(m)
+            vector_share(m)
+            if m:
+                banks[m - 1] = product(m - 1)
+            else:
+                quantise(k_codes[:, FUSED], k_scales[:, FUSED], k_fused)
+                quantise(k_codes[:, PLAIN], k_scales[:, PLAIN], k_plain)
+        banks[TILES - 1] = product(TILES - 1)
+        for m in range(TILES):
             empty(nc.scalar.copy if m < 2 else nc.vector.tensor_copy, m, 0)
             if m >= 2:
                 empty(nc.scalar.copy, m, 1)
-            nc.sync.dma_start(out[0, P * m : P * (m + 1), :], res[m])
+            store(m)

@@ -1,6 +1,7 @@
 from contextlib import ExitStack
 
 import concourse.mybir as mybir
+from concourse.masks import make_identity
 
 D, C, N, Q = 512, 512, 256, 512
 
@@ -15,15 +16,14 @@ COPY = mybir.ActivationFunctionType.Copy
 
 P = 128
 PLANES = 4
-BLOCK = 32
 LIST_ROWS = 16
 RUN = 4
 HALF = N // 2
 TILES = Q // P
 FUSED, PLAIN = slice(0, HALF), slice(HALF, N)
-VECTOR_SHARES = (32, 56, 48, 72)
+VECTOR_SHARES = (56, 40, 48, 72)
 EDGE = 4
-BORDERS = (2, 3)
+BORDERS = ()
 FLOPS = 2 * D * Q * N
 
 
@@ -33,28 +33,25 @@ def tile_attend_pq_lin_kernel(tc, qT, cb, norm, offs, out):
         keep = ctx.enter_context(tc.tile_pool(name="keep", bufs=1))
         psum = ctx.enter_context(tc.psum_pool(name="psum", bufs=1))
 
-        def tile(name, cols, dtype):
-            return keep.tile([P, cols], dtype, name=name, align_bytes=256)
+        def tile(name, cols, dtype, tag=None):
+            return keep.tile([P, cols], dtype, name=name, tag=tag or name, align_bytes=256)
 
         offsets = tile("offsets", N // LIST_ROWS, U16)
-        norm_rows = tile("norm_rows", BLOCK, F32)
-        norm_cols = tile("norm_cols", BLOCK, F32)
-        norm_wide = {h: tile(f"norm_wide{h}", HALF, F32) for h in range(2)}
-        norm_t = {h: tile(f"norm_t{h}", HALF, F32) for h in range(2)}
+        norm_pairs = tile("norm_pairs", N // P, F32)
+        identity = tile("identity", P, F32)
+        q_rows = tile("q_rows", PLANES * Q, BF16)[:]
+        row32 = q_rows.bitcast(F32)
+        norm_fused = row32[:, P // 2 : P // 2 + HALF]
         books = [tile(f"book{t}", C, F32) for t in range(PLANES)]
         raw = tile("raw", PLANES * Q, F32)
-        scaled = tile("scaled", PLANES * HALF, F32)[:].rearrange("p (t n) -> p t n", t=PLANES)
-        plain = tile("plain", PLANES * HALF, BF16)[:].rearrange("p (t n) -> p t n", t=PLANES)
-        early = tile("early", HALF, F32)
+        scaled = row32[:, 3 * P : 3 * P + PLANES * HALF].rearrange("p (t n) -> p t n", t=PLANES)
         k_fused = tile("k_fused", PLANES * HALF, BF16)[:]
         k_plain = tile("k_plain", PLANES * HALF, BF16)[:]
-        q_rows = tile("q_rows", PLANES * Q, BF16)[:]
         k_codes = tile("k_codes", N, U32)
         k_scales = tile("k_scales", N, U8)
         q_codes = [tile(f"q_codes{m}", P, U32) for m in range(TILES)]
         q_scales = [tile(f"q_scales{m}", P, U8) for m in range(TILES)]
-        res = [raw[:, Q * m + P : Q * m + 3 * P] for m in range(2)]
-        res += [tile(f"res{m}", N, F32)[:] for m in (2, 3)]
+        res = [tile(f"res{m}", N, F32)[:] for m in range(TILES)]
 
         def runs(planes):
             return planes.rearrange("p t (c i) -> p c t i", i=RUN)
@@ -115,7 +112,7 @@ def tile_attend_pq_lin_kernel(tc, qT, cb, norm, offs, out):
         cb_planes = cb.rearrange("(p t) c -> p t c", t=PLANES)
         q_pairs = qT[0].rearrange("(p u e) q -> p u (e q)", u=2, e=2)
         raw_pairs = raw[:].rearrange("p (u x) -> p u x", u=2)
-        nc.sync.dma_start(norm_rows[:], norm[0 : P * BLOCK // N, :].rearrange("r (b y) -> (r b) y", y=BLOCK))
+        nc.sync.dma_start(norm_pairs[:], norm[0, :].rearrange("(p j) -> p j", p=P))
         nc.sync.dma_start(books[0][:], cb_planes[:, 0, :])
         nc.sync.dma_start(offsets[:], offs)
         for t in range(1, PLANES):
@@ -124,37 +121,39 @@ def tile_attend_pq_lin_kernel(tc, qT, cb, norm, offs, out):
             part = slice(Q + P * m if m else 0, Q + P * (m + 1))
             nc.sync.dma_start(raw_pairs[:, :, part], q_pairs[:, :, part])
 
-        nc.vector.transpose(norm_cols[:], norm_rows[:])
-        for h, copy in ((0, nc.vector.tensor_copy), (1, nc.vector.tensor_copy)):
-            squares = slice(h * HALF // BLOCK, (h + 1) * HALF // BLOCK)
-            copy(
-                out=norm_wide[h][:].rearrange("p (b x) -> p b x", x=BLOCK),
-                in_=norm_cols[:, squares].unsqueeze(2).to_broadcast([P, HALF // BLOCK, BLOCK]),
-            )
-        for h in range(2):
-            nc.vector.transpose(norm_t[h][:], norm_wide[h][:])
+        make_identity(nc, identity[:])
+        norm_bank = psum.tile([P, N // P, P], F32, name="norm_bank")
+        for j in range(N // P):
+            nc.tensor.transpose(norm_bank[:, j, :], norm_pairs[:, j : j + 1].to_broadcast([P, P]), identity[:])
+        nc.scalar.copy(
+            out=norm_fused.rearrange("p (x j) -> p x j", j=N // P),
+            in_=norm_bank[:, :, : P // 2].rearrange("p j x -> p x j"),
+        )
 
-        nc.vector.tensor_copy(early[:], books[0][:].indirect(entries(PLAIN)))
-        nc.scalar.copy(out=plain[:, 0, :], in_=early[:])
+        plain = tile("plain", PLANES * HALF, BF16, tag="identity")[:].rearrange("p (t n) -> p t n", t=PLANES)
+        nc.vector.tensor_copy(plain[:, 0, :], books[0][:].indirect(entries(PLAIN)))
         for t in range(PLANES):
             if t:
                 nc.scalar.activation(plain[:, t, :], books[t][:].indirect(entries(PLAIN)), COPY)
-            nc.vector.tensor_tensor(scaled[:, t, :], books[t][:].indirect(entries(FUSED)), norm_t[0][:], MULT)
+            nc.vector.tensor_tensor(scaled[:, t, :], books[t][:].indirect(entries(FUSED)), norm_fused, MULT)
         nc.scalar.copy(out=words(k_fused), in_=runs(scaled))
-        spread = norm_t[1][:].rearrange("p (c i) -> p c i", i=RUN).unsqueeze(2)
+        spread = norm_bank[:, :, P // 2 :].rearrange("p j x -> p x j").unsqueeze(2)
         nc.vector.tensor_tensor(
-            words(k_plain), runs(plain), spread.to_broadcast([P, HALF // RUN, PLANES, RUN]), MULT
+            k_plain.rearrange("p (x j t) -> p x t j", j=N // P, t=PLANES),
+            plain.rearrange("p t (x j) -> p x t j", j=N // P),
+            spread.to_broadcast([P, P // 2, PLANES, N // P]),
+            MULT,
         )
 
         banks = {}
         for m in range(TILES):
             scalar_share(m)
             vector_share(m)
+            if m < 2:
+                cols = (FUSED, PLAIN)[m]
+                quantise(k_codes[:, cols], k_scales[:, cols], (k_fused, k_plain)[m])
             if m:
                 banks[m - 1] = product(m - 1)
-            else:
-                quantise(k_codes[:, FUSED], k_scales[:, FUSED], k_fused)
-                quantise(k_codes[:, PLAIN], k_scales[:, PLAIN], k_plain)
         banks[TILES - 1] = product(TILES - 1)
         for m in range(TILES):
             empty(nc.scalar.copy if m < 2 else nc.vector.tensor_copy, m, 0)

@@ -72,7 +72,7 @@ def tile_attend_pq_lin_kernel(tc, qT, cb, norm, offs, out):
         def product(m):
             quantise(q_codes[m][:], q_scales[m][:], q_rows[:, PLANES * P * m : PLANES * P * (m + 1)])
             banks = []
-            for cols in (FUSED, PLAIN) if m >= 2 else (slice(0, N),):
+            for cols in (slice(0, N),) if m in (1, 2) else (FUSED, PLAIN):
                 acc = psum.tile([P, cols.stop - cols.start], F32, name=f"acc{m}_{cols.start}")
                 nc.tensor.matmul_mx(
                     out=acc[:],
@@ -130,12 +130,14 @@ def tile_attend_pq_lin_kernel(tc, qT, cb, norm, offs, out):
             in_=norm_bank[:, :, : P // 2].rearrange("p j x -> p x j"),
         )
 
-        plain = tile("plain", PLANES * HALF, BF16, tag="identity")[:].rearrange("p (t n) -> p t n", t=PLANES)
-        nc.vector.tensor_copy(plain[:, 0, :], books[0][:].indirect(entries(PLAIN)))
-        for t in range(PLANES):
-            if t:
-                nc.scalar.activation(plain[:, t, :], books[t][:].indirect(entries(PLAIN)), COPY)
+        picked = tile("picked", HALF + PLANES * HALF, BF16, tag="identity")
+        plain = picked[:, HALF:].rearrange("p (t n) -> p t n", t=PLANES)
+        nc.vector.tensor_copy(picked[:, :N], books[0][:].indirect(offsets[:]))
+        for t in range(1, PLANES):
+            nc.scalar.activation(plain[:, t, :], books[t][:].indirect(entries(PLAIN)), COPY)
             nc.vector.tensor_tensor(scaled[:, t, :], books[t][:].indirect(entries(FUSED)), norm_fused, MULT)
+            if t == 1:
+                nc.vector.tensor_tensor(scaled[:, 0, :], picked[:, :HALF], norm_fused, MULT)
         nc.scalar.copy(out=words(k_fused), in_=runs(scaled))
         spread = norm_bank[:, :, P // 2 :].rearrange("p j x -> p x j").unsqueeze(2)
         nc.vector.tensor_tensor(
@@ -149,14 +151,14 @@ def tile_attend_pq_lin_kernel(tc, qT, cb, norm, offs, out):
         for m in range(TILES):
             scalar_share(m)
             vector_share(m)
-            if m < 2:
-                cols = (FUSED, PLAIN)[m]
-                quantise(k_codes[:, cols], k_scales[:, cols], (k_fused, k_plain)[m])
             if m:
                 banks[m - 1] = product(m - 1)
+            else:
+                quantise(k_codes[:, FUSED], k_scales[:, FUSED], k_fused)
+                quantise(k_codes[:, PLAIN], k_scales[:, PLAIN], k_plain)
         banks[TILES - 1] = product(TILES - 1)
         for m in range(TILES):
             empty(nc.scalar.copy if m < 2 else nc.vector.tensor_copy, m, 0)
-            if m >= 2:
+            if m not in (1, 2):
                 empty(nc.scalar.copy, m, 1)
             store(m)

from contextlib import ExitStack

import concourse.mybir as mybir
from concourse.masks import make_identity

D, C, N, Q = 512, 512, 256, 512

F32 = mybir.dt.float32
BF16 = mybir.dt.bfloat16
U16 = mybir.dt.uint16
U32 = mybir.dt.uint32
U8 = mybir.dt.uint8
FP8X4 = mybir.dt.float8_e4m3fn_x4
MULT = mybir.AluOpType.mult
COPY = mybir.ActivationFunctionType.Copy

P = 128
PLANES = 4
LIST_ROWS = 16
RUN = 4
HALF = N // 2
TILES = Q // P
FUSED, PLAIN = slice(0, HALF), slice(HALF, N)
VECTOR_SHARES = (56, 40, 48, 72)
EDGE = 4
BORDERS = ()
FLOPS = 2 * D * Q * N


def tile_attend_pq_lin_kernel(tc, qT, cb, norm, offs, out):
    nc = tc.nc
    with ExitStack() as ctx:
        keep = ctx.enter_context(tc.tile_pool(name="keep", bufs=1))
        psum = ctx.enter_context(tc.psum_pool(name="psum", bufs=1))

        def tile(name, cols, dtype, tag=None):
            return keep.tile([P, cols], dtype, name=name, tag=tag or name, align_bytes=256)

        offsets = tile("offsets", N // LIST_ROWS, U16)
        norm_pairs = tile("norm_pairs", N // P, F32)
        identity = tile("identity", P, F32)
        q_rows = tile("q_rows", PLANES * Q, BF16)[:]
        row32 = q_rows.bitcast(F32)
        norm_fused = row32[:, P // 2 : P // 2 + HALF]
        books = [tile(f"book{t}", C, F32) for t in range(PLANES)]
        raw = tile("raw", PLANES * Q, F32)
        scaled = row32[:, 3 * P : 3 * P + PLANES * HALF].rearrange("p (t n) -> p t n", t=PLANES)
        k_fused = tile("k_fused", PLANES * HALF, BF16)[:]
        k_plain = tile("k_plain", PLANES * HALF, BF16)[:]
        k_codes = tile("k_codes", N, U32)
        k_scales = tile("k_scales", N, U8)
        q_codes = [tile(f"q_codes{m}", P, U32) for m in range(TILES)]
        q_scales = [tile(f"q_scales{m}", P, U8) for m in range(TILES)]
        res = [tile(f"res{m}", N, F32)[:] for m in range(TILES)]

        def runs(planes):
            return planes.rearrange("p t (c i) -> p c t i", i=RUN)

        def words(values):
            return values.rearrange("p (c i t) -> p c t i", i=RUN, t=PLANES)

        def interleave_q(copy, a, b):
            planes = raw[:].rearrange("p (t q) -> p t q", t=PLANES)
            copy(out=words(q_rows[:, PLANES * a : PLANES * b]), in_=runs(planes[:, :, a:b]))

        def entries(cols):
            return offsets[:, cols.start // LIST_ROWS : cols.stop // LIST_ROWS]

        def quantise(codes, scales, values):
            nc.vector.quantize_mx(out=codes.bitcast(FP8X4), scales=scales, in_=values)

        def product(m):
            quantise(q_codes[m][:], q_scales[m][:], q_rows[:, PLANES * P * m : PLANES * P * (m + 1)])
            banks = []
            for cols in (slice(0, N),) if m in (1, 2) else (FUSED, PLAIN):
                acc = psum.tile([P, cols.stop - cols.start], F32, name=f"acc{m}_{cols.start}")
                nc.tensor.matmul_mx(
                    out=acc[:],
                    lhsT=q_codes[m][:].bitcast(FP8X4),
                    lhsT_scale=q_scales[m][:],
                    rhs=k_codes[:, cols].bitcast(FP8X4),
                    rhs_scale=k_scales[:, cols],
                    start=True,
                    stop=True,
                )
                banks.append((cols, acc))
            return banks

        def empty(copy, m, half):
            cols, acc = banks[m][half]
            copy(out=res[m][:, cols], in_=acc[:])

        def store(m):
            nc.sync.dma_start(out[0, P * m : P * (m + 1), :], res[m])

        def scalar_share(m):
            lo = P * m
            if m in BORDERS:
                interleave_q(nc.scalar.copy, lo - EDGE, lo + EDGE)
                lo = lo + EDGE
            interleave_q(nc.scalar.copy, lo, cut(m))

        def end(m):
            return P * (m + 1) - (EDGE if m + 1 in BORDERS else 0)

        def cut(m):
            return end(m) - VECTOR_SHARES[m]

        def vector_share(m):
            interleave_q(nc.vector.tensor_copy, cut(m), end(m))

        cb_planes = cb.rearrange("(p t) c -> p t c", t=PLANES)
        q_pairs = qT[0].rearrange("(p u e) q -> p u (e q)", u=2, e=2)
        raw_pairs = raw[:].rearrange("p (u x) -> p u x", u=2)
        nc.sync.dma_start(norm_pairs[:], norm[0, :].rearrange("(p j) -> p j", p=P))
        nc.sync.dma_start(books[0][:], cb_planes[:, 0, :])
        nc.sync.dma_start(offsets[:], offs)
        for t in range(1, PLANES):
            nc.sync.dma_start(books[t][:], cb_planes[:, t, :])
        for m in range(TILES):
            part = slice(Q + P * m if m else 0, Q + P * (m + 1))
            nc.sync.dma_start(raw_pairs[:, :, part], q_pairs[:, :, part])

        make_identity(nc, identity[:])
        norm_bank = psum.tile([P, N // P, P], F32, name="norm_bank")
        for j in range(N // P):
            nc.tensor.transpose(norm_bank[:, j, :], norm_pairs[:, j : j + 1].to_broadcast([P, P]), identity[:])
        nc.scalar.copy(
            out=norm_fused.rearrange("p (x j) -> p x j", j=N // P),
            in_=norm_bank[:, :, : P // 2].rearrange("p j x -> p x j"),
        )

        picked = tile("picked", HALF + PLANES * HALF, BF16, tag="identity")
        plain = picked[:, HALF:].rearrange("p (t n) -> p t n", t=PLANES)
        nc.vector.tensor_copy(picked[:, :N], books[0][:].indirect(offsets[:]))
        for t in range(1, PLANES):
            nc.scalar.activation(plain[:, t, :], books[t][:].indirect(entries(PLAIN)), COPY)
            nc.vector.tensor_tensor(scaled[:, t, :], books[t][:].indirect(entries(FUSED)), norm_fused, MULT)
            if t == 1:
                nc.vector.tensor_tensor(scaled[:, 0, :], picked[:, :HALF], norm_fused, MULT)
        nc.scalar.copy(out=words(k_fused), in_=runs(scaled))
        spread = norm_bank[:, :, P // 2 :].rearrange("p j x -> p x j").unsqueeze(2)
        nc.vector.tensor_tensor(
            k_plain.rearrange("p (x j t) -> p x t j", j=N // P, t=PLANES),
            plain.rearrange("p t (x j) -> p x t j", j=N // P),
            spread.to_broadcast([P, P // 2, PLANES, N // P]),
            MULT,
        )

        banks = {}
        for m in range(TILES):
            scalar_share(m)
            vector_share(m)
            if m:
                banks[m - 1] = product(m - 1)
            else:
                quantise(k_codes[:, FUSED], k_scales[:, FUSED], k_fused)
                quantise(k_codes[:, PLAIN], k_scales[:, PLAIN], k_plain)
        banks[TILES - 1] = product(TILES - 1)
        for m in range(TILES):
            empty(nc.scalar.copy if m < 2 else nc.vector.tensor_copy, m, 0)
            if m not in (1, 2):
                empty(nc.scalar.copy, m, 1)
            store(m)
